import numpy as np
import ml_dtypes


def mxq(x, axis, fmt="e4m3"):
    dtype, down = {"e4m3": (ml_dtypes.float8_e4m3fn, 7), "e5m2": (ml_dtypes.float8_e5m2, 14)}[fmt]
    v = np.moveaxis(np.asarray(x, np.float32).astype(ml_dtypes.bfloat16).astype(np.float64), axis, -1)
    blocks = v.reshape(v.shape[:-1] + (-1, 32))
    amax = np.abs(blocks).max(-1, keepdims=True)
    byte = np.maximum(np.where(amax > 0, np.frexp(amax)[1] - 1 + 127, 0) - down, 1)
    scale = np.exp2(byte - 127.0)
    codes = (blocks / scale).astype(np.float32).astype(dtype).astype(np.float64)
    return np.moveaxis((codes * scale).reshape(v.shape), -1, axis)


WIDE = False


def mx_kscale(k):
    if not WIDE:
        return np.ones(k)
    levels = np.array([10, -10, 5, -5, 0])
    if k % 512:
        return np.exp2(np.random.permutation(np.resize(levels, k // 32))).repeat(32)
    a = np.empty((k // 512, 16))
    for p in range(k // 512):
        a[p, :8] = np.random.permutation(np.resize(levels, 8))
        for g in range(8):
            far = levels[np.abs(levels - a[p, g]) >= 10]
            a[p, g + 8] = far[np.random.randint(len(far))]
    return np.exp2(a.ravel()).repeat(32)


def f64(x):
    return np.asarray(x).astype(np.float64)


def striped(idx):
    return np.tile(np.asarray(idx).reshape(-1, 16).T, (8, 1)).astype(np.uint16)


def unstriped(offs):
    return offs[:16].T.reshape(-1).astype(np.int64)


B, N, T, D, DV, NQ = 2, 512, 2048, 512, 256, 256
PAGE = 64
CAP = 2.0


def setup_inputs():
    n = np.random.standard_normal
    pages = np.random.permutation(T // PAGE)[:B * N // PAGE]
    idx = (pages[:, None] * PAGE + np.arange(PAGE)[None, :]).reshape(-1)
    s = mx_kscale(D)[:, None]
    u = np.ones(T)
    u[idx] = mx_kscale(B * N)
    r = np.random.uniform(0.5, 2.0, T)
    rk = np.random.uniform(0.5, 2.0, T)
    k = n((D, T)) / s / rk
    v = n((DV, T)) / (u * r)
    return {
        "qT": (n((B, D, NQ)) * s * (0.80 / np.sqrt(D))).astype(np.float32),
        "kT": k.astype(np.float32),
        "vT": v.astype(np.float32),
        "ks": np.tile(rk, (128, 1)).astype(np.float32),
        "vs": np.tile(u * r, (128, 1)).astype(np.float32),
        "offs": striped(idx),
    }


def reference(qT, kT, vT, ks, vs, offs):
    idx = unstriped(offs)
    k = f64(kT)
    v = f64(vT)
    pick = lambda x: x[:, idx].reshape(x.shape[0], B, N).transpose(1, 0, 2)
    q = f64(qT)
    score = mxq(q, 1, "e4m3").transpose(0, 2, 1) @ mxq(pick(k), 1, "e4m3")
    score = score * pick(f64(ks))[:, :1, :]
    score = CAP * np.tanh(score / CAP)
    m = score.max(-1, keepdims=True)
    p = np.exp(score - m)
    total = p.sum(-1, keepdims=True)
    w = p * pick(f64(vs))[:, :1, :]
    y = mxq(w, 2, "e4m3") @ mxq(pick(v).transpose(0, 2, 1), 1, "e4m3")
    y = y / total
    return y

@@ -1,0 +1,256 @@
+from contextlib import ExitStack
+
+import concourse.mybir as mybir
+from concourse.masks import make_identity
+
+B, N, T, D, DV, NQ = 2, 512, 2048, 512, 256, 256
+P = 128
+PACK = 4
+CAP = 2.0
+
+FLOPS = 2 * B * NQ * N * (D + DV)
+BYTES = 4 * (B * D * NQ + D * T + DV * T + 2 * T + B * NQ * DV) + 2 * B * N * P // 16
+
+F32 = mybir.dt.float32
+BF16 = mybir.dt.bfloat16
+U32 = mybir.dt.uint32
+U16 = mybir.dt.uint16
+U8 = mybir.dt.uint8
+FP8X4 = mybir.dt.float8_e4m3fn_x4
+
+MULT = mybir.AluOpType.mult
+MIN = mybir.AluOpType.min
+COPY = mybir.ActivationFunctionType.Copy
+EXP = mybir.ActivationFunctionType.Exp
+TANH = mybir.ActivationFunctionType.Tanh
+
+
+def tile_attend_x_ks_cap_kernel(tc, qT, kT, vT, ks, vs, offs, out):
+    nc = tc.nc
+    with ExitStack() as ctx:
+        held = ctx.enter_context(tc.tile_pool(name="held", bufs=1))
+        work = ctx.enter_context(tc.tile_pool(name="work", bufs=2))
+        psum = ctx.enter_context(tc.psum_pool(name="psum", bufs=2))
+
+        offsets = held.tile([P, B * N // 16], U16, name="offsets")
+        nc.sync.dma_start(offsets[:], offs)
+
+        ks_pool = held.tile([P, T], F32, name="ks_pool")
+        vs_pool = held.tile([P, T], F32, name="vs_pool")
+        nc.vector.memset(ks_pool[:], 0.0)
+        warm = held.tile([P, 8], F32, name="warm")
+        nc.vector.memset(warm[:], 0.0)
+        nc.vector.memset(vs_pool[:], 0.0)
+        nc.scalar.activation(warm[:, 0:1], warm[:, 1:2], EXP)
+        ident_f = held.tile([P, P], F32, name="ident_f")
+        make_identity(nc, ident_f[:])
+        ident_b = held.tile([P, P], BF16, name="ident_b")
+        make_identity(nc, ident_b[:])
+
+        q_raw, k_pool, v_pool = [], [], []
+        for b in range(B):
+            q_raw.append(held.tile([P, PACK, NQ], F32, name=f"q_raw{b}"))
+        for j in range(PACK):
+            k_pool.append(held.tile([P, T], F32, name=f"k_pool{j}"))
+        for h in range(2):
+            v_pool.append(held.tile([P, T], F32, name=f"v_pool{h}"))
+        k_rows = kT.rearrange("(p j) w -> p j w", j=PACK)
+        nc.sync.dma_start(k_pool[0][:], k_rows[:, 0, :])
+        nc.sync.dma_start(ks_pool[0:1, :], ks[0:1, :])
+        nc.sync.dma_start(k_pool[1][:], k_rows[:, 1, :])
+        nc.sync.dma_start(vs_pool[0:1, :], vs[0:1, :])
+        for j in range(2, PACK):
+            nc.sync.dma_start(k_pool[j][:], k_rows[:, j, :])
+        for b in range(B):
+            nc.sync.dma_start(q_raw[b][:], qT[b].rearrange("(p j) w -> p j w", j=PACK))
+        for h in range(2):
+            nc.sync.dma_start(v_pool[h][:], vT[h * P : (h + 1) * P, :])
+
+        q_codes, q_scales = [], []
+        k_codes, k_scales = [], []
+        w_codes, w_scales = [], []
+        v_codes, v_scales = [], []
+        q_in, k_in, v_in, w_in = [], [], [], []
+        out_ps, total, inverse, y = [], [], [], []
+        for b in range(B):
+            q_in.append(held.tile([P, NQ, PACK], BF16, name=f"q_in{b}", align_bytes=64))
+            k_in.append(held.tile([P, N, PACK], BF16, name=f"k_in{b}", align_bytes=64))
+            v_in.append(held.tile([P, DV, PACK], BF16, name=f"v_in{b}", align_bytes=64))
+            w_in.append(held.tile([P, NQ, PACK], BF16, name=f"w_in{b}", align_bytes=64))
+            q_codes.append(held.tile([P, NQ], U32, name=f"q_codes{b}", align_bytes=64))
+            q_scales.append(held.tile([P, NQ], U8, name=f"q_scales{b}", align_bytes=64))
+            k_codes.append(held.tile([P, N], U32, name=f"k_codes{b}", align_bytes=64))
+            k_scales.append(held.tile([P, N], U8, name=f"k_scales{b}", align_bytes=64))
+            w_codes.append(held.tile([P, NQ], U32, name=f"w_codes{b}", align_bytes=64))
+            w_scales.append(held.tile([P, NQ], U8, name=f"w_scales{b}", align_bytes=64))
+            v_codes.append(held.tile([P, DV], U32, name=f"v_codes{b}", align_bytes=64))
+            v_scales.append(held.tile([P, DV], U8, name=f"v_scales{b}", align_bytes=64))
+            total.append(held.tile([P, 2], F32, name=f"total{b}"))
+            inverse.append(held.tile([P, 2], F32, name=f"inverse{b}"))
+            y.append(held.tile([P, 2, DV], F32, name=f"y{b}"))
+            out_ps.append(psum.tile([P, 2, DV], F32, name=f"out_ps{b}", tag="O", bufs=2))
+        ks_got = held.tile([P, B * N], F32, name="ks_got")
+        vs_got = held.tile([P, B * N], F32, name="vs_got")
+        ks_col = held.tile([P, 8], F32, name="ks_col")
+        vs_col = held.tile([P, 8], F32, name="vs_col")
+        vs_row = held.tile([P, B * N], F32, name="vs_row")
+        k_got = held.tile([P, PACK, B * N], F32, name="k_got")
+        v_got = []
+        for h in range(2):
+            v_got.append(held.tile([P, B * N], F32, name=f"v_got{h}"))
+
+        def slots(b):
+            return slice(b * N, (b + 1) * N)
+
+        def entries(b):
+            return offsets[:, b * (N // 16) : (b + 1) * (N // 16)]
+
+        def quantize(codes, scales, cols, grouped):
+            nc.vector.quantize_mx(
+                out=codes[:, cols].bitcast(FP8X4),
+                scales=scales[:, cols],
+                in_=grouped[:, cols, :].rearrange("p c j -> p (c j)"),
+            )
+
+        def columns(got, col, factor):
+            for b in range(B):
+                turned = psum.tile([P, 4, P], F32, name="turned", tag="tT")
+                for m in range(4):
+                    nc.tensor.transpose(turned[:, m, :], got[:, (4 * b + m) * P : (4 * b + m + 1) * P], ident_f[:])
+                nc.scalar.activation(col[:, 4 * b : 4 * b + 4], turned[:, :, 0], COPY, scale=factor)
+
+        def spread_vs():
+            for b in range(B):
+                spread = psum.tile([P, 4, P], F32, name="spread", tag="tT")
+                for m in range(4):
+                    nc.tensor.transpose(spread[:, m, :], vs_col[:, 4 * b + m : 4 * b + m + 1].to_broadcast([P, P]), ident_f[:])
+                nc.scalar.copy(vs_row[:, slots(b)], spread[:].rearrange("p m s -> p (m s)"))
+
+        def group_q(b):
+            nc.scalar.copy(q_in[b][:], q_raw[b][:].rearrange("p j c -> p c j"))
+
+        def group_k(engine, b, j):
+            engine(k_in[b][:, :, j : j + 2], k_got[:, j : j + 2, slots(b)].rearrange("p j c -> p c j"))
+
+        def scores(b):
+            th = work.tile([P, 4, NQ], F32, name="th")
+            for g in range(2):
+                s_ps = psum.tile([P, 2, NQ], F32, name="s_ps", tag="S", bufs=2)
+                for i in range(2):
+                    m = 2 * g + i
+                    cols = slice(m * P, (m + 1) * P)
+                    nc.tensor.matmul_mx(
+                        out=s_ps[:, i, :],
+                        lhsT=k_codes[b][:, cols].bitcast(FP8X4),
+                        lhsT_scale=k_scales[b][:, cols],
+                        rhs=q_codes[b][:].bitcast(FP8X4),
+                        rhs_scale=q_scales[b][:],
+                        start=True,
+                        stop=True,
+                    )
+                    nc.scalar.activation(th[:, m, :], s_ps[:, i, :], TANH, scale=ks_col[:, 4 * b + m : 4 * b + m + 1])
+            return th
+
+        def soften(b, t, th):
+            tT = psum.tile([P, N], F32, name="tT", tag="tT")
+            for m in range(4):
+                nc.tensor.transpose(tT[:, m * P : (m + 1) * P], th[:, m, t * P : (t + 1) * P], ident_f[:])
+            minus_c = work.tile([P, N], F32, name="minus_c")
+            minus_m = work.tile([P, 1], F32, name="minus_m")
+            nc.vector.tensor_scalar(minus_c[:], tT[:], -CAP, None, MULT, MIN, accum_out=minus_m[:])
+            p = work.tile([P, N], F32, name="p")
+            nc.scalar.activation(p[:], tT[:], EXP, bias=minus_m[:], scale=CAP, accum_out=total[b][:, t : t + 1])
+            return p
+
+        def weigh(b, t, p):
+            w = work.tile([P, N], BF16, name="w")
+            nc.vector.tensor_tensor(w[:], p[:], vs_row[:, slots(b)], MULT)
+            wT = psum.tile([P, PACK, P], BF16, name="wT", tag="wT", bufs=1)
+            for j in range(PACK):
+                nc.tensor.transpose(wT[:, j, :], w[:, j::PACK], ident_b[:])
+            nc.scalar.copy(w_in[b][:, t * P : (t + 1) * P, :], wT[:].rearrange("p j c -> p c j"))
+
+        def quant_w(b, t):
+            quantize(w_codes[b], w_scales[b], slice(t * P, (t + 1) * P), w_in[b])
+
+        def gather_v(h, b):
+            nc.vector.tensor_copy(v_got[h][:, slots(b)], v_pool[h][:].indirect(entries(b)))
+
+        def turn_v(h, b):
+            vT_ps = psum.tile([P, PACK, P], F32, name="vT_ps", tag="vT", bufs=1)
+            for j in range(PACK):
+                nc.tensor.transpose(vT_ps[:, j, :], v_got[h][:, b * N + j : (b + 1) * N : PACK], ident_f[:])
+            nc.scalar.copy(v_in[b][:, h * P : (h + 1) * P, :], vT_ps[:].rearrange("p j c -> p c j"))
+
+        def quant_v(h, b):
+            quantize(v_codes[b], v_scales[b], slice(h * P, (h + 1) * P), v_in[b])
+
+        def product(b, t):
+            rows = slice(t * P, (t + 1) * P)
+            nc.tensor.matmul_mx(
+                out=out_ps[b][:, t, :],
+                lhsT=w_codes[b][:, rows].bitcast(FP8X4),
+                lhsT_scale=w_scales[b][:, rows],
+                rhs=v_codes[b][:].bitcast(FP8X4),
+                rhs_scale=v_scales[b][:],
+                start=True,
+                stop=True,
+            )
+            if (b, t) == (1, 1):
+                nc.vector.tensor_scalar(y[b][:, t, :], out_ps[b][:, t, :], inverse[b][:, t : t + 1], None, MULT)
+            else:
+                nc.scalar.activation(y[b][:, t, :], out_ps[b][:, t, :], COPY, scale=inverse[b][:, t : t + 1])
+            nc.sync.dma_start(out[b, rows, :], y[b][:, t, :])
+
+        def gather_k(j):
+            nc.vector.tensor_copy(k_got[:, j, :], k_pool[j][:].indirect(offsets[:]))
+
+        gather_k(0)
+        nc.vector.tensor_copy(ks_got[:], ks_pool[:].indirect(offsets[:]))
+        gather_k(1)
+        columns(ks_got, ks_col, 1.0 / CAP)
+        for b in range(B):
+            group_k(nc.scalar.copy, b, 0)
+        nc.vector.tensor_copy(vs_got[:], vs_pool[:].indirect(offsets[:]))
+        gather_k(2)
+        for b in range(B):
+            nc.vector.tensor_copy(k_got[:, 3, slots(b)], k_pool[3][:].indirect(entries(b)))
+        group_k(nc.vector.tensor_copy, 0, 2)
+        group_q(0)
+        columns(vs_got, vs_col, 1.0)
+        spread_vs()
+        group_q(1)
+        quantize(k_codes[0], k_scales[0], slice(0, N), k_in[0])
+        quantize(q_codes[0], q_scales[0], slice(0, NQ), q_in[0])
+        th0 = scores(0)
+        group_k(nc.vector.tensor_copy, 1, 2)
+        quantize(q_codes[1], q_scales[1], slice(0, NQ), q_in[1])
+        quantize(k_codes[1], k_scales[1], slice(0, N), k_in[1])
+        nc.vector.tensor_copy(v_got[0][:], v_pool[0][:].indirect(offsets[:]))
+        th1 = scores(1)
+        p00 = soften(0, 0, th0)
+        p01 = soften(0, 1, th0)
+        turn_v(0, 0)
+        gather_v(1, 0)
+        weigh(0, 0, p00)
+        p10 = soften(1, 0, th1)
+        turn_v(0, 1)
+        weigh(0, 1, p01)
+        p11 = soften(1, 1, th1)
+        nc.vector.reciprocal(inverse[0][:], total[0][:])
+        weigh(1, 0, p10)
+        turn_v(1, 0)
+        gather_v(1, 1)
+        quantize(w_codes[0], w_scales[0], slice(0, NQ), w_in[0])
+        weigh(1, 1, p11)
+        nc.vector.reciprocal(inverse[1][:], total[1][:])
+        quantize(v_codes[0], v_scales[0], slice(0, DV), v_in[0])
+        turn_v(1, 1)
+        product(0, 0)
+        product(0, 1)
+        quant_w(1, 0)
+        quant_v(0, 1)
+        quant_v(1, 1)
+        product(1, 0)
+        quant_w(1, 1)
+        product(1, 1)

@@ -44,23 +44,31 @@ def tile_attend_x_ks_cap_kernel(tc, qT, kT, vT, ks, vs, offs, out):
         nc.scalar.activation(warm[:, 0:1], warm[:, 1:2], EXP)
         ident_f = held.tile([P, P], F32, name="ident_f")
         make_identity(nc, ident_f[:])
-        ident_b = held.tile([P, P], BF16, name="ident_b")
-        make_identity(nc, ident_b[:])
 
-        q_raw, k_pool, v_pool = [], [], []
+        k_rows = kT.rearrange("(p h j) w -> p h j w", h=2, j=2)
+        cuts = [[0, 512, 1024, 1536, 2048], [0, 512, 1024, 1408, 2048]]
+        k_raw = [[], []]
+        for h in range(2):
+            for c in range(len(cuts[h]) - 1):
+                k_raw[h].append(held.tile([P, 2, cuts[h][c + 1] - cuts[h][c]], F32, name=f"k_raw{h}_{c}"))
+        q_raw, v_pool, k_pair = [], [], []
         for b in range(B):
             q_raw.append(held.tile([P, PACK, NQ], F32, name=f"q_raw{b}"))
-        for j in range(PACK):
-            k_pool.append(held.tile([P, T], F32, name=f"k_pool{j}"))
         for h in range(2):
             v_pool.append(held.tile([P, T], F32, name=f"v_pool{h}"))
-        k_rows = kT.rearrange("(p j) w -> p j w", j=PACK)
-        nc.sync.dma_start(k_pool[0][:], k_rows[:, 0, :])
+            k_pair.append(held.tile([P, 2 * T], BF16, name=f"k_pair{h}", align_bytes=64))
+
+        def load_k(h, c):
+            nc.sync.dma_start(k_raw[h][c][:], k_rows[:, h, :, cuts[h][c] : cuts[h][c + 1]])
+
+        load_k(0, 0)
         nc.sync.dma_start(ks_pool[0:1, :], ks[0:1, :])
-        nc.sync.dma_start(k_pool[1][:], k_rows[:, 1, :])
+        load_k(0, 1)
         nc.sync.dma_start(vs_pool[0:1, :], vs[0:1, :])
-        for j in range(2, PACK):
-            nc.sync.dma_start(k_pool[j][:], k_rows[:, j, :])
+        for c in range(2, len(k_raw[0])):
+            load_k(0, c)
+        for c in range(len(k_raw[1])):
+            load_k(1, c)
         for b in range(B):
             nc.sync.dma_start(q_raw[b][:], qT[b].rearrange("(p j) w -> p j w", j=PACK))
         for h in range(2):
@@ -71,12 +79,12 @@ def tile_attend_x_ks_cap_kernel(tc, qT, kT, vT, ks, vs, offs, out):
         w_codes, w_scales = [], []
         v_codes, v_scales = [], []
         q_in, k_in, v_in, w_in = [], [], [], []
-        out_ps, total, inverse, y = [], [], [], []
+        total, inverse, y, v_got = [], [], [], []
         for b in range(B):
             q_in.append(held.tile([P, NQ, PACK], BF16, name=f"q_in{b}", align_bytes=64))
-            k_in.append(held.tile([P, N, PACK], BF16, name=f"k_in{b}", align_bytes=64))
-            v_in.append(held.tile([P, DV, PACK], BF16, name=f"v_in{b}", align_bytes=64))
-            w_in.append(held.tile([P, NQ, PACK], BF16, name=f"w_in{b}", align_bytes=64))
+            k_in.append(held.tile([P, N * PACK], BF16, name=f"k_in{b}", align_bytes=64))
+            v_in.append(held.tile([P, DV * PACK], BF16, name=f"v_in{b}", align_bytes=64))
+            w_in.append([held.tile([P, P, PACK], BF16, name=f"w_in{b}_{t}", align_bytes=64) for t in range(2)])
             q_codes.append(held.tile([P, NQ], U32, name=f"q_codes{b}", align_bytes=64))
             q_scales.append(held.tile([P, NQ], U8, name=f"q_scales{b}", align_bytes=64))
             k_codes.append(held.tile([P, N], U32, name=f"k_codes{b}", align_bytes=64))
@@ -87,55 +95,60 @@ def tile_attend_x_ks_cap_kernel(tc, qT, kT, vT, ks, vs, offs, out):
             v_scales.append(held.tile([P, DV], U8, name=f"v_scales{b}", align_bytes=64))
             total.append(held.tile([P, 2], F32, name=f"total{b}"))
             inverse.append(held.tile([P, 2], F32, name=f"inverse{b}"))
-            y.append(held.tile([P, 2, DV], F32, name=f"y{b}"))
-            out_ps.append(psum.tile([P, 2, DV], F32, name=f"out_ps{b}", tag="O", bufs=2))
+            y.append([held.tile([P, DV], F32, name=f"y{b}_{t}") for t in range(2)])
+            v_got.append([held.tile([P, N], BF16, name=f"v_got{b}_{h}", align_bytes=64) for h in range(2)])
         ks_got = held.tile([P, B * N], F32, name="ks_got")
         vs_got = held.tile([P, B * N], F32, name="vs_got")
-        ks_col = held.tile([P, 8], F32, name="ks_col")
-        vs_col = held.tile([P, 8], F32, name="vs_col")
-        vs_row = held.tile([P, B * N], F32, name="vs_row")
-        k_got = held.tile([P, PACK, B * N], F32, name="k_got")
-        v_got = []
-        for h in range(2):
-            v_got.append(held.tile([P, B * N], F32, name=f"v_got{h}"))
-
-        def slots(b):
-            return slice(b * N, (b + 1) * N)
 
         def entries(b):
             return offsets[:, b * (N // 16) : (b + 1) * (N // 16)]
 
-        def quantize(codes, scales, cols, grouped):
-            nc.vector.quantize_mx(
-                out=codes[:, cols].bitcast(FP8X4),
-                scales=scales[:, cols],
-                in_=grouped[:, cols, :].rearrange("p c j -> p (c j)"),
-            )
+        def quantize(codes, scales, grouped):
+            nc.vector.quantize_mx(out=codes.bitcast(FP8X4), scales=scales, in_=grouped)
 
-        def columns(got, col, factor):
+        def ks_columns():
+            ks_col = held.tile([P, B * 4], F32, name="ks_col", tag="k_raw1_2")
             for b in range(B):
                 turned = psum.tile([P, 4, P], F32, name="turned", tag="tT")
                 for m in range(4):
-                    nc.tensor.transpose(turned[:, m, :], got[:, (4 * b + m) * P : (4 * b + m + 1) * P], ident_f[:])
-                nc.scalar.activation(col[:, 4 * b : 4 * b + 4], turned[:, :, 0], COPY, scale=factor)
+                    nc.tensor.transpose(turned[:, m, :], ks_got[:, (4 * b + m) * P : (4 * b + m + 1) * P], ident_f[:])
+                nc.scalar.activation(ks_col[:, 4 * b : 4 * b + 4], turned[:, :, 0], COPY, scale=1.0 / CAP)
+            return ks_col
 
-        def spread_vs():
+        def vs_columns():
+            vs_col = held.tile([P, B * 4], F32, name="vs_col", tag="q_raw1")
             for b in range(B):
-                spread = psum.tile([P, 4, P], F32, name="spread", tag="tT")
-                for m in range(4):
-                    nc.tensor.transpose(spread[:, m, :], vs_col[:, 4 * b + m : 4 * b + m + 1].to_broadcast([P, P]), ident_f[:])
-                nc.scalar.copy(vs_row[:, slots(b)], spread[:].rearrange("p m s -> p (m s)"))
+                turned = psum.tile([P, 4, P], F32, name="turned", tag="tT")
+                for j in range(PACK):
+                    nc.tensor.transpose(turned[:, j, :], vs_got[:, b * N + j : (b + 1) * N : PACK], ident_f[:])
+                nc.scalar.copy(vs_col[:, 4 * b : 4 * b + 4], turned[:, :, 0])
+            return vs_col
+
+        def cast_k(h, c):
+            lo, hi = cuts[h][c], cuts[h][c + 1]
+            copy = nc.vector.tensor_copy if (h, c) == (1, 3) else nc.scalar.copy
+            copy(
+                k_pair[h][:, 2 * lo : 2 * hi].rearrange("p (w j) -> p w j", j=2),
+                k_raw[h][c][:].rearrange("p j w -> p w j"),
+            )
+
+        def gather_k(h, b):
+            words = k_in[b][:].bitcast(U32).rearrange("p (s h) -> p s h", h=2)
+            nc.vector.tensor_copy(words[:, :, h], k_pair[h][:].bitcast(U32).indirect(entries(b)))
 
         def group_q(b):
             nc.scalar.copy(q_in[b][:], q_raw[b][:].rearrange("p j c -> p c j"))
 
-        def group_k(engine, b, j):
-            engine(k_in[b][:, :, j : j + 2], k_got[:, j : j + 2, slots(b)].rearrange("p j c -> p c j"))
+        def quant_q(b):
+            quantize(q_codes[b][:], q_scales[b][:], q_in[b][:].rearrange("p c j -> p (c j)"))
+
+        def quant_k(b):
+            quantize(k_codes[b][:], k_scales[b][:], k_in[b][:])
 
         def scores(b):
             th = work.tile([P, 4, NQ], F32, name="th")
             for g in range(2):
-                s_ps = psum.tile([P, 2, NQ], F32, name="s_ps", tag="S", bufs=2)
+                s_ps = psum.tile([P, 2, NQ], F32, name="s_ps", tag="S")
                 for i in range(2):
                     m = 2 * g + i
                     cols = slice(m * P, (m + 1) * P)
@@ -148,6 +161,8 @@ def tile_attend_x_ks_cap_kernel(tc, qT, kT, vT, ks, vs, offs, out):
                         start=True,
                         stop=True,
                     )
+                for i in range(2):
+                    m = 2 * g + i
                     nc.scalar.activation(th[:, m, :], s_ps[:, i, :], TANH, scale=ks_col[:, 4 * b + m : 4 * b + m + 1])
             return th
 
@@ -155,40 +170,52 @@ def tile_attend_x_ks_cap_kernel(tc, qT, kT, vT, ks, vs, offs, out):
             tT = psum.tile([P, N], F32, name="tT", tag="tT")
             for m in range(4):
                 nc.tensor.transpose(tT[:, m * P : (m + 1) * P], th[:, m, t * P : (t + 1) * P], ident_f[:])
-            minus_c = work.tile([P, N], F32, name="minus_c")
+            minus_c = work.tile([P, PACK, P], F32, name="minus_c")
             minus_m = work.tile([P, 1], F32, name="minus_m")
-            nc.vector.tensor_scalar(minus_c[:], tT[:], -CAP, None, MULT, MIN, accum_out=minus_m[:])
-            p = work.tile([P, N], F32, name="p")
-            nc.scalar.activation(p[:], tT[:], EXP, bias=minus_m[:], scale=CAP, accum_out=total[b][:, t : t + 1])
+            nc.vector.tensor_scalar(
+                minus_c[:], tT[:].rearrange("p (s j) -> p j s", j=PACK), -CAP, None, MULT, MIN, accum_out=minus_m[:]
+            )
+            p = work.tile([P, PACK, P], F32, name="p")
+            nc.scalar.activation(p[:], minus_c[:], EXP, bias=minus_m[:], scale=-1.0, accum_out=total[b][:, t : t + 1])
             return p
 
         def weigh(b, t, p):
-            w = work.tile([P, N], BF16, name="w")
-            nc.vector.tensor_tensor(w[:], p[:], vs_row[:, slots(b)], MULT)
-            wT = psum.tile([P, PACK, P], BF16, name="wT", tag="wT", bufs=1)
+            pT = psum.tile([P, PACK, P], F32, name="pT", tag="pT")
             for j in range(PACK):
-                nc.tensor.transpose(wT[:, j, :], w[:, j::PACK], ident_b[:])
-            nc.scalar.copy(w_in[b][:, t * P : (t + 1) * P, :], wT[:].rearrange("p j c -> p c j"))
+                nc.tensor.transpose(pT[:, j, :], p[:, j, :], ident_f[:])
+            nc.vector.tensor_tensor(
+                w_in[b][t][:],
+                pT[:].rearrange("p j c -> p c j"),
+                vs_col[:, 4 * b : 4 * b + 4].unsqueeze(1).to_broadcast([P, P, PACK]),
+                MULT,
+            )
 
         def quant_w(b, t):
-            quantize(w_codes[b], w_scales[b], slice(t * P, (t + 1) * P), w_in[b])
+            rows = slice(t * P, (t + 1) * P)
+            quantize(w_codes[b][:, rows], w_scales[b][:, rows], w_in[b][t][:].rearrange("p c j -> p (c j)"))
 
         def gather_v(h, b):
-            nc.vector.tensor_copy(v_got[h][:, slots(b)], v_pool[h][:].indirect(entries(b)))
+            nc.vector.tensor_copy(v_got[b][h][:], v_pool[h][:].indirect(entries(b)))
 
-        def turn_v(h, b):
-            vT_ps = psum.tile([P, PACK, P], F32, name="vT_ps", tag="vT", bufs=1)
-            for j in range(PACK):
-                nc.tensor.transpose(vT_ps[:, j, :], v_got[h][:, b * N + j : (b + 1) * N : PACK], ident_f[:])
-            nc.scalar.copy(v_in[b][:, h * P : (h + 1) * P, :], vT_ps[:].rearrange("p j c -> p c j"))
+        def turn_v(b):
+            vT_ps = psum.tile([P, 2, 2, P], F32, name="vT_ps", tag="vT", bufs=1)
+            for h in range(2):
+                words = v_got[b][h][:].bitcast(F32)
+                for u in range(2):
+                    nc.tensor.transpose(vT_ps[:, h, u, :], words[:, u::2], ident_f[:])
+            nc.scalar.copy(
+                v_in[b][:].bitcast(F32).rearrange("p (h e u) -> p h e u", h=2, u=2),
+                vT_ps[:].rearrange("p h u e -> p h e u"),
+            )
 
-        def quant_v(h, b):
-            quantize(v_codes[b], v_scales[b], slice(h * P, (h + 1) * P), v_in[b])
+        def quant_v(b):
+            quantize(v_codes[b][:], v_scales[b][:], v_in[b][:])
 
         def product(b, t):
             rows = slice(t * P, (t + 1) * P)
+            out_ps = psum.tile([P, DV], F32, name="out_ps", tag="S")
             nc.tensor.matmul_mx(
-                out=out_ps[b][:, t, :],
+                out=out_ps[:],
                 lhsT=w_codes[b][:, rows].bitcast(FP8X4),
                 lhsT_scale=w_scales[b][:, rows],
                 rhs=v_codes[b][:].bitcast(FP8X4),
@@ -196,61 +223,52 @@ def tile_attend_x_ks_cap_kernel(tc, qT, kT, vT, ks, vs, offs, out):
                 start=True,
                 stop=True,
             )
-            if (b, t) == (1, 1):
-                nc.vector.tensor_scalar(y[b][:, t, :], out_ps[b][:, t, :], inverse[b][:, t : t + 1], None, MULT)
-            else:
-                nc.scalar.activation(y[b][:, t, :], out_ps[b][:, t, :], COPY, scale=inverse[b][:, t : t + 1])
-            nc.sync.dma_start(out[b, rows, :], y[b][:, t, :])
+            nc.scalar.activation(y[b][t][:], out_ps[:], COPY, scale=inverse[b][:, t : t + 1])
+            nc.sync.dma_start(out[b, rows, :], y[b][t][:])
 
-        def gather_k(j):
-            nc.vector.tensor_copy(k_got[:, j, :], k_pool[j][:].indirect(offsets[:]))
-
-        gather_k(0)
+        for c in range(len(k_raw[0])):
+            cast_k(0, c)
         nc.vector.tensor_copy(ks_got[:], ks_pool[:].indirect(offsets[:]))
-        gather_k(1)
-        columns(ks_got, ks_col, 1.0 / CAP)
-        for b in range(B):
-            group_k(nc.scalar.copy, b, 0)
         nc.vector.tensor_copy(vs_got[:], vs_pool[:].indirect(offsets[:]))
-        gather_k(2)
         for b in range(B):
-            nc.vector.tensor_copy(k_got[:, 3, slots(b)], k_pool[3][:].indirect(entries(b)))
-        group_k(nc.vector.tensor_copy, 0, 2)
+            gather_k(0, b)
+        for c in range(len(k_raw[1])):
+            cast_k(1, c)
+        gather_k(1, 0)
         group_q(0)
-        columns(vs_got, vs_col, 1.0)
-        spread_vs()
-        group_q(1)
-        quantize(k_codes[0], k_scales[0], slice(0, N), k_in[0])
-        quantize(q_codes[0], q_scales[0], slice(0, NQ), q_in[0])
+        ks_col = ks_columns()
+        quant_k(0)
+        quant_q(0)
+        gather_k(1, 1)
         th0 = scores(0)
-        group_k(nc.vector.tensor_copy, 1, 2)
-        quantize(q_codes[1], q_scales[1], slice(0, NQ), q_in[1])
-        quantize(k_codes[1], k_scales[1], slice(0, N), k_in[1])
-        nc.vector.tensor_copy(v_got[0][:], v_pool[0][:].indirect(offsets[:]))
-        th1 = scores(1)
+        group_q(1)
+        vs_col = vs_columns()
+        quant_k(1)
+        quant_q(1)
         p00 = soften(0, 0, th0)
         p01 = soften(0, 1, th0)
-        turn_v(0, 0)
-        gather_v(1, 0)
+        th1 = scores(1)
+        gather_v(0, 0)
         weigh(0, 0, p00)
-        p10 = soften(1, 0, th1)
-        turn_v(0, 1)
         weigh(0, 1, p01)
+        p10 = soften(1, 0, th1)
         p11 = soften(1, 1, th1)
+        gather_v(1, 0)
+        turn_v(0)
+        quant_w(0, 0)
+        quant_w(0, 1)
         nc.vector.reciprocal(inverse[0][:], total[0][:])
-        weigh(1, 0, p10)
-        turn_v(1, 0)
+        gather_v(0, 1)
         gather_v(1, 1)
-        quantize(w_codes[0], w_scales[0], slice(0, NQ), w_in[0])
-        weigh(1, 1, p11)
-        nc.vector.reciprocal(inverse[1][:], total[1][:])
-        quantize(v_codes[0], v_scales[0], slice(0, DV), v_in[0])
-        turn_v(1, 1)
+        quant_v(0)
+        turn_v(1)
         product(0, 0)
         product(0, 1)
+        weigh(1, 0, p10)
+        nc.vector.reciprocal(inverse[1][:], total[1][:])
+        quant_v(1)
+        weigh(1, 1, p11)
         quant_w(1, 0)
-        quant_v(0, 1)
-        quant_v(1, 1)
         product(1, 0)
         quant_w(1, 1)
         product(1, 1)

@@ -14,6 +14,7 @@ BYTES = 4 * (B * D * NQ + D * T + DV * T + 2 * T + B * NQ * DV) + 2 * B * N * P 
 F32 = mybir.dt.float32
 BF16 = mybir.dt.bfloat16
 U32 = mybir.dt.uint32
+I32 = mybir.dt.int32
 U16 = mybir.dt.uint16
 U8 = mybir.dt.uint8
 FP8X4 = mybir.dt.float8_e4m3fn_x4
@@ -40,20 +41,21 @@ def tile_attend_x_ks_cap_kernel(tc, qT, kT, vT, ks, vs, offs, out):
         nc.vector.memset(ks_pool[:], 0.0)
         warm = held.tile([P, 8], F32, name="warm")
         nc.vector.memset(warm[:], 0.0)
-        nc.vector.memset(vs_pool[:], 0.0)
+        nc.gpsimd.memset(vs_pool[:], 0.0)
         nc.scalar.activation(warm[:, 0:1], warm[:, 1:2], EXP)
         ident_f = held.tile([P, P], F32, name="ident_f")
         make_identity(nc, ident_f[:])
 
         k_rows = kT.rearrange("(p h j) w -> p h j w", h=2, j=2)
-        cuts = [[0, 512, 1024, 1536, 2048], [0, 512, 1024, 1408, 2048]]
+        cuts = [[0, 1024, 2048], [0, 1024, 2048]]
+        split = 384
         k_raw = [[], []]
         for h in range(2):
             for c in range(len(cuts[h]) - 1):
-                k_raw[h].append(held.tile([P, 2, cuts[h][c + 1] - cuts[h][c]], F32, name=f"k_raw{h}_{c}"))
+                k_raw[h].append(held.tile([P, 2, cuts[h][c + 1] - cuts[h][c]], F32, name=f"k_raw{h}_{c}", align_bytes=64))
         q_raw, v_pool, k_pair = [], [], []
         for b in range(B):
-            q_raw.append(held.tile([P, PACK, NQ], F32, name=f"q_raw{b}"))
+            q_raw.append(held.tile([P, PACK, NQ], F32, name=f"q_raw{b}", align_bytes=64))
         for h in range(2):
             v_pool.append(held.tile([P, T], F32, name=f"v_pool{h}"))
             k_pair.append(held.tile([P, 2 * T], BF16, name=f"k_pair{h}", align_bytes=64))
@@ -62,10 +64,9 @@ def tile_attend_x_ks_cap_kernel(tc, qT, kT, vT, ks, vs, offs, out):
             nc.sync.dma_start(k_raw[h][c][:], k_rows[:, h, :, cuts[h][c] : cuts[h][c + 1]])
 
         load_k(0, 0)
-        nc.sync.dma_start(ks_pool[0:1, :], ks[0:1, :])
-        load_k(0, 1)
         nc.sync.dma_start(vs_pool[0:1, :], vs[0:1, :])
-        for c in range(2, len(k_raw[0])):
+        nc.sync.dma_start(ks_pool[0:1, :], ks[0:1, :])
+        for c in range(1, len(k_raw[0])):
             load_k(0, c)
         for c in range(len(k_raw[1])):
             load_k(1, c)
@@ -81,7 +82,6 @@ def tile_attend_x_ks_cap_kernel(tc, qT, kT, vT, ks, vs, offs, out):
         q_in, k_in, v_in, w_in = [], [], [], []
         total, inverse, y, v_got = [], [], [], []
         for b in range(B):
-            q_in.append(held.tile([P, NQ, PACK], BF16, name=f"q_in{b}", align_bytes=64))
             k_in.append(held.tile([P, N * PACK], BF16, name=f"k_in{b}", align_bytes=64))
             v_in.append(held.tile([P, DV * PACK], BF16, name=f"v_in{b}", align_bytes=64))
             w_in.append([held.tile([P, P, PACK], BF16, name=f"w_in{b}_{t}", align_bytes=64) for t in range(2)])
@@ -96,7 +96,8 @@ def tile_attend_x_ks_cap_kernel(tc, qT, kT, vT, ks, vs, offs, out):
             total.append(held.tile([P, 2], F32, name=f"total{b}"))
             inverse.append(held.tile([P, 2], F32, name=f"inverse{b}"))
             y.append([held.tile([P, DV], F32, name=f"y{b}_{t}") for t in range(2)])
-            v_got.append([held.tile([P, N], BF16, name=f"v_got{b}_{h}", align_bytes=64) for h in range(2)])
+            v_got.append([])
+        k_got = [held.tile([P, 2, N], U32, name=f"k_got{b}") for b in range(B)]
         ks_got = held.tile([P, B * N], F32, name="ks_got")
         vs_got = held.tile([P, B * N], F32, name="vs_got")
 
@@ -107,7 +108,7 @@ def tile_attend_x_ks_cap_kernel(tc, qT, kT, vT, ks, vs, offs, out):
             nc.vector.quantize_mx(out=codes.bitcast(FP8X4), scales=scales, in_=grouped)
 
         def ks_columns():
-            ks_col = held.tile([P, B * 4], F32, name="ks_col", tag="k_raw1_2")
+            ks_col = held.tile([P, B * 4], F32, name="ks_col", tag="k_raw1_0", align_bytes=64)
             for b in range(B):
                 turned = psum.tile([P, 4, P], F32, name="turned", tag="tT")
                 for m in range(4):
@@ -116,7 +117,7 @@ def tile_attend_x_ks_cap_kernel(tc, qT, kT, vT, ks, vs, offs, out):
             return ks_col
 
         def vs_columns():
-            vs_col = held.tile([P, B * 4], F32, name="vs_col", tag="q_raw1")
+            vs_col = held.tile([P, B * 4], F32, name="vs_col", tag="q_raw1", align_bytes=64)
             for b in range(B):
                 turned = psum.tile([P, 4, P], F32, name="turned", tag="tT")
                 for j in range(PACK):
@@ -124,20 +125,24 @@ def tile_attend_x_ks_cap_kernel(tc, qT, kT, vT, ks, vs, offs, out):
                 nc.scalar.copy(vs_col[:, 4 * b : 4 * b + 4], turned[:, :, 0])
             return vs_col
 
-        def cast_k(h, c):
-            lo, hi = cuts[h][c], cuts[h][c + 1]
-            copy = nc.vector.tensor_copy if (h, c) == (1, 3) else nc.scalar.copy
+        def cast_k(copy, h, c, lo, hi):
+            base = cuts[h][c]
             copy(
-                k_pair[h][:, 2 * lo : 2 * hi].rearrange("p (w j) -> p w j", j=2),
-                k_raw[h][c][:].rearrange("p j w -> p w j"),
+                k_pair[h][:, 2 * (base + lo) : 2 * (base + hi)].rearrange("p (w j) -> p w j", j=2),
+                k_raw[h][c][:, :, lo:hi].rearrange("p j w -> p w j"),
             )
 
         def gather_k(h, b):
-            words = k_in[b][:].bitcast(U32).rearrange("p (s h) -> p s h", h=2)
-            nc.vector.tensor_copy(words[:, :, h], k_pair[h][:].bitcast(U32).indirect(entries(b)))
+            nc.vector.tensor_copy(k_got[b][:, h, :], k_pair[h][:].bitcast(U32).indirect(entries(b)))
+
+        def group_k(b):
+            words = k_in[b][:].bitcast(I32).rearrange("p (s h) -> p s h", h=2)
+            nc.vector.tensor_copy(words, k_got[b][:].bitcast(I32).rearrange("p h s -> p s h"))
 
         def group_q(b):
-            nc.scalar.copy(q_in[b][:], q_raw[b][:].rearrange("p j c -> p c j"))
+            grouped = held.tile([P, NQ, PACK], BF16, name="grouped", tag=["k_raw1_1", "q_raw0"][b], align_bytes=64)
+            nc.scalar.copy(grouped[:], q_raw[b][:].rearrange("p j c -> p c j"))
+            q_in.append(grouped)
 
         def quant_q(b):
             quantize(q_codes[b][:], q_scales[b][:], q_in[b][:].rearrange("p c j -> p (c j)"))
@@ -195,7 +200,10 @@ def tile_attend_x_ks_cap_kernel(tc, qT, kT, vT, ks, vs, offs, out):
             quantize(w_codes[b][:, rows], w_scales[b][:, rows], w_in[b][t][:].rearrange("p c j -> p (c j)"))
 
         def gather_v(h, b):
-            nc.vector.tensor_copy(v_got[b][h][:], v_pool[h][:].indirect(entries(b)))
+            tag = f"k_in{b}" if h == 0 else f"v_got{b}"
+            got = held.tile([P, N], BF16, name="got", tag=tag, align_bytes=64)
+            nc.vector.tensor_copy(got[:], v_pool[h][:].indirect(entries(b)))
+            v_got[b].append(got)
 
         def turn_v(b):
             vT_ps = psum.tile([P, 2, 2, P], F32, name="vT_ps", tag="vT", bufs=1)
@@ -226,20 +234,23 @@ def tile_attend_x_ks_cap_kernel(tc, qT, kT, vT, ks, vs, offs, out):
             nc.scalar.activation(y[b][t][:], out_ps[:], COPY, scale=inverse[b][:, t : t + 1])
             nc.sync.dma_start(out[b, rows, :], y[b][t][:])
 
-        for c in range(len(k_raw[0])):
-            cast_k(0, c)
-        nc.vector.tensor_copy(ks_got[:], ks_pool[:].indirect(offsets[:]))
+        for c in range(2):
+            cast_k(nc.scalar.copy, 0, c, 0, 1024)
         nc.vector.tensor_copy(vs_got[:], vs_pool[:].indirect(offsets[:]))
+        nc.vector.tensor_copy(ks_got[:], ks_pool[:].indirect(offsets[:]))
         for b in range(B):
             gather_k(0, b)
-        for c in range(len(k_raw[1])):
-            cast_k(1, c)
+        cast_k(nc.scalar.copy, 1, 0, 0, 1024)
+        cast_k(nc.scalar.copy, 1, 1, 0, split)
+        cast_k(nc.vector.tensor_copy, 1, 1, split, 1024)
         gather_k(1, 0)
+        group_k(0)
         group_q(0)
         ks_col = ks_columns()
         quant_k(0)
         quant_q(0)
         gather_k(1, 1)
+        group_k(1)
         th0 = scores(0)
         group_q(1)
         vs_col = vs_columns()

@@ -7,6 +7,9 @@ B, N, T, D, DV, NQ = 2, 512, 2048, 512, 256, 256
 P = 128
 PACK = 4
 CAP = 2.0
+RUN = 4
+CHUNK = T // 2
+SPLIT = 384
 
 FLOPS = 2 * B * NQ * N * (D + DV)
 BYTES = 4 * (B * D * NQ + D * T + DV * T + 2 * T + B * NQ * DV) + 2 * B * N * P // 16
@@ -14,7 +17,6 @@ BYTES = 4 * (B * D * NQ + D * T + DV * T + 2 * T + B * NQ * DV) + 2 * B * N * P 
 F32 = mybir.dt.float32
 BF16 = mybir.dt.bfloat16
 U32 = mybir.dt.uint32
-I32 = mybir.dt.int32
 U16 = mybir.dt.uint16
 U8 = mybir.dt.uint8
 FP8X4 = mybir.dt.float8_e4m3fn_x4
@@ -30,76 +32,54 @@ def tile_attend_x_ks_cap_kernel(tc, qT, kT, vT, ks, vs, offs, out):
     nc = tc.nc
     with ExitStack() as ctx:
         held = ctx.enter_context(tc.tile_pool(name="held", bufs=1))
-        work = ctx.enter_context(tc.tile_pool(name="work", bufs=2))
-        psum = ctx.enter_context(tc.psum_pool(name="psum", bufs=2))
+        psum = ctx.enter_context(tc.psum_pool(name="psum", bufs=1))
+
+        def sbuf(shape, dtype, place):
+            return held.tile(shape, dtype, name=place, tag=place, align_bytes=64)
 
         offsets = held.tile([P, B * N // 16], U16, name="offsets")
-        nc.sync.dma_start(offsets[:], offs)
 
-        ks_pool = held.tile([P, T], F32, name="ks_pool")
-        vs_pool = held.tile([P, T], F32, name="vs_pool")
+        ks_pool = sbuf([P, T], F32, "ks_pool")
+        vs_pool = sbuf([P, T], F32, "vs_pool")
         nc.vector.memset(ks_pool[:], 0.0)
-        warm = held.tile([P, 8], F32, name="warm")
-        nc.vector.memset(warm[:], 0.0)
         nc.gpsimd.memset(vs_pool[:], 0.0)
-        nc.scalar.activation(warm[:, 0:1], warm[:, 1:2], EXP)
-        ident_f = held.tile([P, P], F32, name="ident_f")
-        make_identity(nc, ident_f[:])
+        identity = sbuf([P, P], F32, "identity")
+        make_identity(nc, identity[:])
 
-        k_rows = kT.rearrange("(p h j) w -> p h j w", h=2, j=2)
-        cuts = [[0, 1024, 2048], [0, 1024, 2048]]
-        split = 384
-        k_raw = [[], []]
-        for h in range(2):
-            for c in range(len(cuts[h]) - 1):
-                k_raw[h].append(held.tile([P, 2, cuts[h][c + 1] - cuts[h][c]], F32, name=f"k_raw{h}_{c}", align_bytes=64))
-        q_raw, v_pool, k_pair = [], [], []
-        for b in range(B):
-            q_raw.append(held.tile([P, PACK, NQ], F32, name=f"q_raw{b}", align_bytes=64))
-        for h in range(2):
-            v_pool.append(held.tile([P, T], F32, name=f"v_pool{h}"))
-            k_pair.append(held.tile([P, 2 * T], BF16, name=f"k_pair{h}", align_bytes=64))
+        k_rows = kT.rearrange("(p h r) w -> p h r w", h=2, r=2)
+        k_raw = [[sbuf([P, 2, CHUNK], F32, f"k_raw{h}{c}") for c in range(2)] for h in range(2)]
+        q_raw = [sbuf([P, PACK, NQ], F32, f"q_raw{b}") for b in range(B)]
+        v_pool = [sbuf([P, T], F32, f"v_pool{e}") for e in range(2)]
+        k_pair = [sbuf([P, 2 * T], BF16, f"k_pair{h}") for h in range(2)]
 
         def load_k(h, c):
-            nc.sync.dma_start(k_raw[h][c][:], k_rows[:, h, :, cuts[h][c] : cuts[h][c + 1]])
+            nc.sync.dma_start(k_raw[h][c][:], k_rows[:, h, :, c * CHUNK : (c + 1) * CHUNK])
 
         load_k(0, 0)
-        nc.sync.dma_start(vs_pool[0:1, :], vs[0:1, :])
+        nc.sync.dma_start(offsets[:], offs)
+        nc.scalar.dma_start(vs_pool[0:1, :], vs[0:1, :])
+        load_k(0, 1)
         nc.sync.dma_start(ks_pool[0:1, :], ks[0:1, :])
-        for c in range(1, len(k_raw[0])):
-            load_k(0, c)
-        for c in range(len(k_raw[1])):
+        for c in range(2):
             load_k(1, c)
         for b in range(B):
             nc.sync.dma_start(q_raw[b][:], qT[b].rearrange("(p j) w -> p j w", j=PACK))
-        for h in range(2):
-            nc.sync.dma_start(v_pool[h][:], vT[h * P : (h + 1) * P, :])
+        for e in range(2):
+            nc.sync.dma_start(v_pool[e][:], vT[e * P : (e + 1) * P, :])
 
-        q_codes, q_scales = [], []
-        k_codes, k_scales = [], []
-        w_codes, w_scales = [], []
-        v_codes, v_scales = [], []
-        q_in, k_in, v_in, w_in = [], [], [], []
-        total, inverse, y, v_got = [], [], [], []
-        for b in range(B):
-            k_in.append(held.tile([P, N * PACK], BF16, name=f"k_in{b}", align_bytes=64))
-            v_in.append(held.tile([P, DV * PACK], BF16, name=f"v_in{b}", align_bytes=64))
-            w_in.append([held.tile([P, P, PACK], BF16, name=f"w_in{b}_{t}", align_bytes=64) for t in range(2)])
-            q_codes.append(held.tile([P, NQ], U32, name=f"q_codes{b}", align_bytes=64))
-            q_scales.append(held.tile([P, NQ], U8, name=f"q_scales{b}", align_bytes=64))
-            k_codes.append(held.tile([P, N], U32, name=f"k_codes{b}", align_bytes=64))
-            k_scales.append(held.tile([P, N], U8, name=f"k_scales{b}", align_bytes=64))
-            w_codes.append(held.tile([P, NQ], U32, name=f"w_codes{b}", align_bytes=64))
-            w_scales.append(held.tile([P, NQ], U8, name=f"w_scales{b}", align_bytes=64))
-            v_codes.append(held.tile([P, DV], U32, name=f"v_codes{b}", align_bytes=64))
-            v_scales.append(held.tile([P, DV], U8, name=f"v_scales{b}", align_bytes=64))
-            total.append(held.tile([P, 2], F32, name=f"total{b}"))
-            inverse.append(held.tile([P, 2], F32, name=f"inverse{b}"))
-            y.append([held.tile([P, DV], F32, name=f"y{b}_{t}") for t in range(2)])
-            v_got.append([])
-        k_got = [held.tile([P, 2, N], U32, name=f"k_got{b}") for b in range(B)]
-        ks_got = held.tile([P, B * N], F32, name="ks_got")
-        vs_got = held.tile([P, B * N], F32, name="vs_got")
+        total = sbuf([P, 2 * B], F32, "total")
+        inverse = sbuf([P, 2 * B], F32, "inverse")
+        k_got = [sbuf([P, 2, N], U32, f"k_got{b}") for b in range(B)]
+        q_codes = [sbuf([P, NQ], U32, f"q_codes{b}") for b in range(B)]
+        k_codes = [sbuf([P, N], U32, f"k_codes{b}") for b in range(B)]
+        w_codes = [sbuf([P, NQ], U32, f"w_codes{b}") for b in range(B)]
+        q_scales = [sbuf([P, NQ], U8, f"q_scales{b}") for b in range(B)]
+        k_scales = [sbuf([P, N], U8, f"k_scales{b}") for b in range(B)]
+        w_scales = [sbuf([P, NQ], U8, f"w_scales{b}") for b in range(B)]
+        v_scales = [sbuf([P, DV], U8, f"v_scales{b}") for b in range(B)]
+        ks_got = sbuf([P, B * N], F32, "ks_got")
+        vs_got = sbuf([P, B * N], F32, "vs_got")
+        q_in, k_in, v_in, v_codes, capped, p_tiles, w_in, v_got = {}, {}, {}, {}, {}, {}, {}, {}
 
         def entries(b):
             return offsets[:, b * (N // 16) : (b + 1) * (N // 16)]
@@ -107,179 +87,188 @@ def tile_attend_x_ks_cap_kernel(tc, qT, kT, vT, ks, vs, offs, out):
         def quantize(codes, scales, grouped):
             nc.vector.quantize_mx(out=codes.bitcast(FP8X4), scales=scales, in_=grouped)
 
-        def ks_columns():
-            ks_col = held.tile([P, B * 4], F32, name="ks_col", tag="k_raw1_0", align_bytes=64)
-            for b in range(B):
-                turned = psum.tile([P, 4, P], F32, name="turned", tag="tT")
-                for m in range(4):
-                    nc.tensor.transpose(turned[:, m, :], ks_got[:, (4 * b + m) * P : (4 * b + m + 1) * P], ident_f[:])
-                nc.scalar.activation(ks_col[:, 4 * b : 4 * b + 4], turned[:, :, 0], COPY, scale=1.0 / CAP)
-            return ks_col
+        def multiply(sums, lhs_codes, lhs_scales, rhs_codes, rhs_scales):
+            nc.tensor.matmul_mx(
+                out=sums,
+                lhsT=lhs_codes.bitcast(FP8X4),
+                lhsT_scale=lhs_scales,
+                rhs=rhs_codes.bitcast(FP8X4),
+                rhs_scale=rhs_scales,
+                start=True,
+                stop=True,
+            )
 
-        def vs_columns():
-            vs_col = held.tile([P, B * 4], F32, name="vs_col", tag="q_raw1", align_bytes=64)
-            for b in range(B):
-                turned = psum.tile([P, 4, P], F32, name="turned", tag="tT")
-                for j in range(PACK):
-                    nc.tensor.transpose(turned[:, j, :], vs_got[:, b * N + j : (b + 1) * N : PACK], ident_f[:])
-                nc.scalar.copy(vs_col[:, 4 * b : 4 * b + 4], turned[:, :, 0])
-            return vs_col
+        def activation_copy(dst, src):
+            nc.scalar.activation(dst, src, COPY)
+
+        def turn_scales(got, bank):
+            turned = psum.tile([P, P + 2 * B * PACK], F32, name="turned", tag=bank)
+            for n in range(B * PACK):
+                b, j = divmod(n, PACK)
+                nc.tensor.transpose(turned[:, 2 * n : 2 * n + P], got[:, b * N + j : (b + 1) * N : PACK], identity[:])
+            return turned
+
+        def scale_columns(turned, factor, place):
+            columns = sbuf([P, B * PACK], F32, place)
+            nc.scalar.activation(columns[:], turned[:, 0 : 2 * B * PACK : 2], COPY, scale=factor)
+            return columns
 
         def cast_k(copy, h, c, lo, hi):
-            base = cuts[h][c]
+            first = c * CHUNK
             copy(
-                k_pair[h][:, 2 * (base + lo) : 2 * (base + hi)].rearrange("p (w j) -> p w j", j=2),
-                k_raw[h][c][:, :, lo:hi].rearrange("p j w -> p w j"),
+                k_pair[h][:, 2 * (first + lo) : 2 * (first + hi)].rearrange("p (w i r) -> p w r i", i=RUN, r=2),
+                k_raw[h][c][:, :, lo:hi].rearrange("p r (w i) -> p w r i", i=RUN),
             )
 
         def gather_k(h, b):
             nc.vector.tensor_copy(k_got[b][:, h, :], k_pair[h][:].bitcast(U32).indirect(entries(b)))
 
-        def group_k(b):
-            words = k_in[b][:].bitcast(I32).rearrange("p (s h) -> p s h", h=2)
-            nc.vector.tensor_copy(words, k_got[b][:].bitcast(I32).rearrange("p h s -> p s h"))
+        def group_k(copy, b, place):
+            k_in[b] = sbuf([P, N * PACK], BF16, place)
+            words = k_in[b][:].bitcast(U32).rearrange("p (j s h) -> p s j h", j=PACK, h=2)
+            copy(words, k_got[b][:].rearrange("p h (s j) -> p s j h", j=PACK))
 
-        def group_q(b):
-            grouped = held.tile([P, NQ, PACK], BF16, name="grouped", tag=["k_raw1_1", "q_raw0"][b], align_bytes=64)
-            nc.scalar.copy(grouped[:], q_raw[b][:].rearrange("p j c -> p c j"))
-            q_in.append(grouped)
+        def group_q(b, place):
+            q_in[b] = sbuf([P, NQ, PACK], BF16, place)
+            nc.scalar.copy(
+                q_in[b][:].rearrange("p (c i) j -> p c j i", i=RUN),
+                q_raw[b][:].rearrange("p j (c i) -> p c j i", i=RUN),
+            )
 
         def quant_q(b):
             quantize(q_codes[b][:], q_scales[b][:], q_in[b][:].rearrange("p c j -> p (c j)"))
 
-        def quant_k(b):
-            quantize(k_codes[b][:], k_scales[b][:], k_in[b][:])
+        def quant_k(b, pieces):
+            width = N // pieces
+            for lo in range(0, N, width):
+                cols = slice(lo, lo + width)
+                quantize(k_codes[b][:, cols], k_scales[b][:, cols], k_in[b][:, PACK * lo : PACK * (lo + width)])
 
         def scores(b):
-            th = work.tile([P, 4, NQ], F32, name="th")
+            capped[b] = sbuf([P, PACK, NQ], F32, f"capped{b}")
             for g in range(2):
-                s_ps = psum.tile([P, 2, NQ], F32, name="s_ps", tag="S")
+                sums = psum.tile([P, 2, NQ], F32, name="sums", tag=f"product{b}{g}")
                 for i in range(2):
-                    m = 2 * g + i
-                    cols = slice(m * P, (m + 1) * P)
-                    nc.tensor.matmul_mx(
-                        out=s_ps[:, i, :],
-                        lhsT=k_codes[b][:, cols].bitcast(FP8X4),
-                        lhsT_scale=k_scales[b][:, cols],
-                        rhs=q_codes[b][:].bitcast(FP8X4),
-                        rhs_scale=q_scales[b][:],
-                        start=True,
-                        stop=True,
-                    )
+                    cols = slice((2 * g + i) * P, (2 * g + i + 1) * P)
+                    multiply(sums[:, i, :], k_codes[b][:, cols], k_scales[b][:, cols], q_codes[b][:], q_scales[b][:])
                 for i in range(2):
-                    m = 2 * g + i
-                    nc.scalar.activation(th[:, m, :], s_ps[:, i, :], TANH, scale=ks_col[:, 4 * b + m : 4 * b + m + 1])
-            return th
+                    n = PACK * b + 2 * g + i
+                    nc.scalar.activation(capped[b][:, 2 * g + i, :], sums[:, i, :], TANH, scale=half_ks[:, n : n + 1])
 
-        def soften(b, t, th):
-            tT = psum.tile([P, N], F32, name="tT", tag="tT")
-            for m in range(4):
-                nc.tensor.transpose(tT[:, m * P : (m + 1) * P], th[:, m, t * P : (t + 1) * P], ident_f[:])
-            minus_c = work.tile([P, PACK, P], F32, name="minus_c")
-            minus_m = work.tile([P, 1], F32, name="minus_m")
-            nc.vector.tensor_scalar(
-                minus_c[:], tT[:].rearrange("p (s j) -> p j s", j=PACK), -CAP, None, MULT, MIN, accum_out=minus_m[:]
-            )
-            p = work.tile([P, PACK, P], F32, name="p")
-            nc.scalar.activation(p[:], minus_c[:], EXP, bias=minus_m[:], scale=-1.0, accum_out=total[b][:, t : t + 1])
-            return p
-
-        def weigh(b, t, p):
-            pT = psum.tile([P, PACK, P], F32, name="pT", tag="pT")
+        def soften(b, t):
+            rows = psum.tile([P, N], F32, name="rows", tag=f"turn{b}{t}")
             for j in range(PACK):
-                nc.tensor.transpose(pT[:, j, :], p[:, j, :], ident_f[:])
+                nc.tensor.transpose(rows[:, j * P : (j + 1) * P], capped[b][:, j, t * P : (t + 1) * P], identity[:])
+            minus_c = sbuf([P, N], F32, f"minus_c{b}{t}")
+            minus_m = sbuf([P, 1], F32, f"minus_m{b}{t}")
+            nc.vector.tensor_scalar(minus_c[:], rows[:], -CAP, None, MULT, MIN, accum_out=minus_m[:])
+            p_tiles[b, t] = sbuf([P, N], F32, f"p{b}{t}")
+            row_sum = total[:, 2 * b + t : 2 * b + t + 1]
+            nc.scalar.activation(p_tiles[b, t][:], minus_c[:], EXP, bias=minus_m[:], scale=-1.0, accum_out=row_sum)
+
+        def weigh(b, t):
+            p_turned = psum.tile([P, PACK, P], F32, name="p_turned", tag=f"product{b}{t}")
+            for j in range(PACK):
+                nc.tensor.transpose(p_turned[:, j, :], p_tiles[b, t][:, j * P : (j + 1) * P], identity[:])
+            w_in[b, t] = sbuf([P, P, PACK], BF16, f"w_in{t}")
+            scales = vs_columns[:, PACK * b : PACK * (b + 1)].unsqueeze(1).unsqueeze(3)
             nc.vector.tensor_tensor(
-                w_in[b][t][:],
-                pT[:].rearrange("p j c -> p c j"),
-                vs_col[:, 4 * b : 4 * b + 4].unsqueeze(1).to_broadcast([P, P, PACK]),
+                w_in[b, t][:].rearrange("p (c i) j -> p c j i", i=RUN),
+                p_turned[:].rearrange("p j (c i) -> p c j i", i=RUN),
+                scales.to_broadcast([P, P // RUN, PACK, RUN]),
                 MULT,
             )
 
         def quant_w(b, t):
-            rows = slice(t * P, (t + 1) * P)
-            quantize(w_codes[b][:, rows], w_scales[b][:, rows], w_in[b][t][:].rearrange("p c j -> p (c j)"))
+            cols = slice(t * P, (t + 1) * P)
+            quantize(w_codes[b][:, cols], w_scales[b][:, cols], w_in[b, t][:].rearrange("p c j -> p (c j)"))
 
-        def gather_v(h, b):
-            tag = f"k_in{b}" if h == 0 else f"v_got{b}"
-            got = held.tile([P, N], BF16, name="got", tag=tag, align_bytes=64)
-            nc.vector.tensor_copy(got[:], v_pool[h][:].indirect(entries(b)))
-            v_got[b].append(got)
+        def gather_v(copy, window, e, b, place):
+            v_got[b, e] = sbuf([P, 2, N // 2], BF16, place)
+            copy(v_got[b, e][:].rearrange("p u (s r) -> p s u r", r=2), window[:].indirect(entries(b)))
 
         def turn_v(b):
-            vT_ps = psum.tile([P, 2, 2, P], F32, name="vT_ps", tag="vT", bufs=1)
-            for h in range(2):
-                words = v_got[b][h][:].bitcast(F32)
+            v_turned = psum.tile([P, 2, 2, P], F32, name="v_turned", tag=f"turn1{b}")
+            for e in range(2):
+                words = v_got[b, e][:].bitcast(F32)
                 for u in range(2):
-                    nc.tensor.transpose(vT_ps[:, h, u, :], words[:, u::2], ident_f[:])
+                    nc.tensor.transpose(v_turned[:, e, u, :], words[:, u, :], identity[:])
+            v_in[b] = sbuf([P, DV * PACK], BF16, f"minus_c1{b}")
             nc.scalar.copy(
-                v_in[b][:].bitcast(F32).rearrange("p (h e u) -> p h e u", h=2, u=2),
-                vT_ps[:].rearrange("p h u e -> p h e u"),
+                v_in[b][:].bitcast(F32).rearrange("p (e c i u) -> p e c u i", e=2, i=2, u=2),
+                v_turned[:].rearrange("p e u (c i) -> p e c u i", i=2),
             )
 
         def quant_v(b):
+            v_codes[b] = sbuf([P, DV], U32, f"p1{b}")
             quantize(v_codes[b][:], v_scales[b][:], v_in[b][:])
 
-        def product(b, t):
-            rows = slice(t * P, (t + 1) * P)
-            out_ps = psum.tile([P, DV], F32, name="out_ps", tag="S")
-            nc.tensor.matmul_mx(
-                out=out_ps[:],
-                lhsT=w_codes[b][:, rows].bitcast(FP8X4),
-                lhsT_scale=w_scales[b][:, rows],
-                rhs=v_codes[b][:].bitcast(FP8X4),
-                rhs_scale=v_scales[b][:],
-                start=True,
-                stop=True,
-            )
-            nc.scalar.activation(y[b][t][:], out_ps[:], COPY, scale=inverse[b][:, t : t + 1])
-            nc.sync.dma_start(out[b, rows, :], y[b][t][:])
+        def divide_on_scalar(dst, sums, factor):
+            nc.scalar.activation(dst, sums, COPY, scale=factor)
 
-        for c in range(2):
-            cast_k(nc.scalar.copy, 0, c, 0, 1024)
+        def divide_on_vector(dst, sums, factor):
+            nc.vector.tensor_scalar(dst, sums, factor, None, MULT)
+
+        def product(divide, b, t):
+            cols = slice(t * P, (t + 1) * P)
+            sums = psum.tile([P, DV], F32, name="sums", tag=f"product{b}{t}")
+            multiply(sums[:], w_codes[b][:, cols], w_scales[b][:, cols], v_codes[b][:], v_scales[b][:])
+            y = sbuf([P, DV], F32, f"y{b}{t}")
+            divide(y[:], sums[:], inverse[:, 2 * b + t : 2 * b + t + 1])
+            nc.sync.dma_start(out[b, cols, :], y[:])
+
+        cast_k(activation_copy, 0, 0, 0, CHUNK)
+        cast_k(nc.scalar.copy, 0, 1, 0, CHUNK)
         nc.vector.tensor_copy(vs_got[:], vs_pool[:].indirect(offsets[:]))
+        vs_turned = turn_scales(vs_got, "turn10")
         nc.vector.tensor_copy(ks_got[:], ks_pool[:].indirect(offsets[:]))
+        ks_turned = turn_scales(ks_got, "turn01")
         for b in range(B):
             gather_k(0, b)
-        cast_k(nc.scalar.copy, 1, 0, 0, 1024)
-        cast_k(nc.scalar.copy, 1, 1, 0, split)
-        cast_k(nc.vector.tensor_copy, 1, 1, split, 1024)
-        gather_k(1, 0)
-        group_k(0)
-        group_q(0)
-        ks_col = ks_columns()
-        quant_k(0)
+        cast_k(nc.scalar.copy, 1, 0, 0, CHUNK)
+        cast_k(nc.scalar.copy, 1, 1, 0, SPLIT)
+        cast_k(nc.vector.tensor_copy, 1, 1, SPLIT, CHUNK)
+
+        for b in range(B):
+            gather_k(1, b)
+        group_q(0, "k_raw11")
+        group_k(nc.vector.tensor_copy, 0, "q_raw0")
+        group_q(1, "q_in1")
+        group_k(nc.scalar.copy, 1, "k_in1")
+        half_ks = scale_columns(ks_turned, 1.0 / CAP, "k_pair1")
+        vs_columns = scale_columns(vs_turned, 1.0, "q_raw1")
         quant_q(0)
-        gather_k(1, 1)
-        group_k(1)
-        th0 = scores(0)
-        group_q(1)
-        vs_col = vs_columns()
-        quant_k(1)
+        quant_k(0, 2)
+        scores(0)
         quant_q(1)
-        p00 = soften(0, 0, th0)
-        p01 = soften(0, 1, th0)
-        th1 = scores(1)
-        gather_v(0, 0)
-        weigh(0, 0, p00)
-        weigh(0, 1, p01)
-        p10 = soften(1, 0, th1)
-        p11 = soften(1, 1, th1)
-        gather_v(1, 0)
+        quant_k(1, 1)
+        scores(1)
+
+        v_half = sbuf([P, T], BF16, "k_in1")
+        nc.vector.tensor_copy(v_half[:], v_pool[0][:])
+        gather_v(activation_copy, v_half, 0, 0, "k_pair1")
+        gather_v(nc.vector.tensor_copy, v_pool[1], 1, 0, "v_got")
+        for t in range(2):
+            soften(0, t)
+        gather_v(activation_copy, v_half, 0, 1, "minus_c01")
+        for t in range(2):
+            soften(1, t)
         turn_v(0)
-        quant_w(0, 0)
-        quant_w(0, 1)
-        nc.vector.reciprocal(inverse[0][:], total[0][:])
-        gather_v(0, 1)
-        gather_v(1, 1)
-        quant_v(0)
+        gather_v(nc.vector.tensor_copy, v_pool[1], 1, 1, "minus_c00")
+
+        for t in range(2):
+            weigh(0, t)
         turn_v(1)
-        product(0, 0)
-        product(0, 1)
-        weigh(1, 0, p10)
-        nc.vector.reciprocal(inverse[1][:], total[1][:])
-        quant_v(1)
-        weigh(1, 1, p11)
+        for t in range(2):
+            quant_w(0, t)
+        weigh(1, 0)
+        nc.vector.reciprocal(inverse[:], total[:])
+        quant_v(0)
+        for t in range(2):
+            product(divide_on_scalar, 0, t)
+        weigh(1, 1)
         quant_w(1, 0)
-        product(1, 0)
+        quant_v(1)
         quant_w(1, 1)
-        product(1, 1)
+        product(divide_on_scalar, 1, 0)
+        product(divide_on_vector, 1, 1)

@@ -8,8 +8,9 @@ P = 128
 PACK = 4
 CAP = 2.0
 RUN = 4
-CHUNK = T // 2
-SPLIT = 384
+KIB = 1024
+CHUNKS = (((0, T // 2), (T // 2, T)), ((0, T // 2), (T // 2, 3 * T // 4), (3 * T // 4, T)))
+SPLIT = 192
 
 FLOPS = 2 * B * NQ * N * (D + DV)
 BYTES = 4 * (B * D * NQ + D * T + DV * T + 2 * T + B * NQ * DV) + 2 * B * N * P // 16
@@ -34,6 +35,12 @@ def tile_attend_x_ks_cap_kernel(tc, qT, kT, vT, ks, vs, offs, out):
         held = ctx.enter_context(tc.tile_pool(name="held", bufs=1))
         psum = ctx.enter_context(tc.psum_pool(name="psum", bufs=1))
 
+        query_bytes = ctx.enter_context(tc.tile_pool(name="query_bytes", bufs=1))
+        last_bytes = ctx.enter_context(tc.tile_pool(name="last_bytes", bufs=1))
+
+        def placed(pool, offset, shape, dtype, name):
+            return pool.tile(shape, dtype, name=name, tag=name, align_bytes=64, offset=offset)
+
         def sbuf(shape, dtype, place):
             return held.tile(shape, dtype, name=place, tag=place, align_bytes=64)
 
@@ -47,20 +54,22 @@ def tile_attend_x_ks_cap_kernel(tc, qT, kT, vT, ks, vs, offs, out):
         make_identity(nc, identity[:])
 
         k_rows = kT.rearrange("(p h r) w -> p h r w", h=2, r=2)
-        k_raw = [[sbuf([P, 2, CHUNK], F32, f"k_raw{h}{c}") for c in range(2)] for h in range(2)]
-        q_raw = [sbuf([P, PACK, NQ], F32, f"q_raw{b}") for b in range(B)]
+        k_raw = [
+            [sbuf([P, 2, hi - lo], F32, f"k_raw{h}{c}") for c, (lo, hi) in enumerate(CHUNKS[h])] for h in range(2)
+        ]
+        q_raw = [placed(query_bytes, 0, [P, PACK, NQ], F32, "q_raw0"), sbuf([P, PACK, NQ], F32, "q_raw1")]
         v_pool = [sbuf([P, T], F32, f"v_pool{e}") for e in range(2)]
         k_pair = [sbuf([P, 2 * T], BF16, f"k_pair{h}") for h in range(2)]
 
         def load_k(h, c):
-            nc.sync.dma_start(k_raw[h][c][:], k_rows[:, h, :, c * CHUNK : (c + 1) * CHUNK])
+            nc.sync.dma_start(k_raw[h][c][:], k_rows[:, h, :, CHUNKS[h][c][0] : CHUNKS[h][c][1]])
 
         load_k(0, 0)
         nc.sync.dma_start(offsets[:], offs)
         nc.scalar.dma_start(vs_pool[0:1, :], vs[0:1, :])
         load_k(0, 1)
         nc.sync.dma_start(ks_pool[0:1, :], ks[0:1, :])
-        for c in range(2):
+        for c in range(len(CHUNKS[1])):
             load_k(1, c)
         for b in range(B):
             nc.sync.dma_start(q_raw[b][:], qT[b].rearrange("(p j) w -> p j w", j=PACK))
@@ -71,7 +80,6 @@ def tile_attend_x_ks_cap_kernel(tc, qT, kT, vT, ks, vs, offs, out):
         inverse = sbuf([P, 2 * B], F32, "inverse")
         k_got = [sbuf([P, 2, N], U32, f"k_got{b}") for b in range(B)]
         q_codes = [sbuf([P, NQ], U32, f"q_codes{b}") for b in range(B)]
-        k_codes = [sbuf([P, N], U32, f"k_codes{b}") for b in range(B)]
         w_codes = [sbuf([P, NQ], U32, f"w_codes{b}") for b in range(B)]
         q_scales = [sbuf([P, NQ], U8, f"q_scales{b}") for b in range(B)]
         k_scales = [sbuf([P, N], U8, f"k_scales{b}") for b in range(B)]
@@ -79,7 +87,7 @@ def tile_attend_x_ks_cap_kernel(tc, qT, kT, vT, ks, vs, offs, out):
         v_scales = [sbuf([P, DV], U8, f"v_scales{b}") for b in range(B)]
         ks_got = sbuf([P, B * N], F32, "ks_got")
         vs_got = sbuf([P, B * N], F32, "vs_got")
-        q_in, k_in, v_in, v_codes, capped, p_tiles, w_in, v_got = {}, {}, {}, {}, {}, {}, {}, {}
+        k_codes, q_in, v_in, v_codes, capped, p_tiles, w_in, v_got = {}, {}, {}, {}, {}, {}, {}, {}
 
         def entries(b):
             return offsets[:, b * (N // 16) : (b + 1) * (N // 16)]
@@ -113,8 +121,9 @@ def tile_attend_x_ks_cap_kernel(tc, qT, kT, vT, ks, vs, offs, out):
             nc.scalar.activation(columns[:], turned[:, 0 : 2 * B * PACK : 2], COPY, scale=factor)
             return columns
 
-        def cast_k(copy, h, c, lo, hi):
-            first = c * CHUNK
+        def cast_k(copy, h, c, lo=0, hi=None):
+            first, end = CHUNKS[h][c]
+            hi = end - first if hi is None else hi
             copy(
                 k_pair[h][:, 2 * (first + lo) : 2 * (first + hi)].rearrange("p (w i r) -> p w r i", i=RUN, r=2),
                 k_raw[h][c][:, :, lo:hi].rearrange("p r (w i) -> p w r i", i=RUN),
@@ -123,10 +132,10 @@ def tile_attend_x_ks_cap_kernel(tc, qT, kT, vT, ks, vs, offs, out):
         def gather_k(h, b):
             nc.vector.tensor_copy(k_got[b][:, h, :], k_pair[h][:].bitcast(U32).indirect(entries(b)))
 
-        def group_k(copy, b, place):
-            k_in[b] = sbuf([P, N * PACK], BF16, place)
+        def group_k(copy, b, blocks):
             words = k_in[b][:].bitcast(U32).rearrange("p (j s h) -> p s j h", j=PACK, h=2)
-            copy(words, k_got[b][:].rearrange("p h (s j) -> p s j h", j=PACK))
+            got = k_got[b][:].rearrange("p h (s j) -> p s j h", j=PACK)
+            copy(words[:, :, blocks, :], got[:, :, blocks, :])
 
         def group_q(b, place):
             q_in[b] = sbuf([P, NQ, PACK], BF16, place)
@@ -138,11 +147,10 @@ def tile_attend_x_ks_cap_kernel(tc, qT, kT, vT, ks, vs, offs, out):
         def quant_q(b):
             quantize(q_codes[b][:], q_scales[b][:], q_in[b][:].rearrange("p c j -> p (c j)"))
 
-        def quant_k(b, pieces):
-            width = N // pieces
-            for lo in range(0, N, width):
-                cols = slice(lo, lo + width)
-                quantize(k_codes[b][:, cols], k_scales[b][:, cols], k_in[b][:, PACK * lo : PACK * (lo + width)])
+        def quant_k(b, g, codes):
+            k_codes[b, g] = codes
+            cols = slice(g * N // 2, (g + 1) * N // 2)
+            quantize(codes[:], k_scales[b][:, cols], k_in[b][:, PACK * cols.start : PACK * cols.stop])
 
         def scores(b):
             capped[b] = sbuf([P, PACK, NQ], F32, f"capped{b}")
@@ -150,50 +158,66 @@ def tile_attend_x_ks_cap_kernel(tc, qT, kT, vT, ks, vs, offs, out):
                 sums = psum.tile([P, 2, NQ], F32, name="sums", tag=f"product{b}{g}")
                 for i in range(2):
                     cols = slice((2 * g + i) * P, (2 * g + i + 1) * P)
-                    multiply(sums[:, i, :], k_codes[b][:, cols], k_scales[b][:, cols], q_codes[b][:], q_scales[b][:])
+                    codes = k_codes[b, g][:, i * P : (i + 1) * P]
+                    multiply(sums[:, i, :], codes, k_scales[b][:, cols], q_codes[b][:], q_scales[b][:])
                 for i in range(2):
                     n = PACK * b + 2 * g + i
                     nc.scalar.activation(capped[b][:, 2 * g + i, :], sums[:, i, :], TANH, scale=half_ks[:, n : n + 1])
 
-        def soften(b, t):
+        def soften(b, t, minus_c):
             rows = psum.tile([P, N], F32, name="rows", tag=f"turn{b}{t}")
             for j in range(PACK):
                 nc.tensor.transpose(rows[:, j * P : (j + 1) * P], capped[b][:, j, t * P : (t + 1) * P], identity[:])
-            minus_c = sbuf([P, N], F32, f"minus_c{b}{t}")
             minus_m = sbuf([P, 1], F32, f"minus_m{b}{t}")
             nc.vector.tensor_scalar(minus_c[:], rows[:], -CAP, None, MULT, MIN, accum_out=minus_m[:])
             p_tiles[b, t] = sbuf([P, N], F32, f"p{b}{t}")
             row_sum = total[:, 2 * b + t : 2 * b + t + 1]
             nc.scalar.activation(p_tiles[b, t][:], minus_c[:], EXP, bias=minus_m[:], scale=-1.0, accum_out=row_sum)
 
-        def weigh(b, t):
+        def turn_p(b, t):
             p_turned = psum.tile([P, PACK, P], F32, name="p_turned", tag=f"product{b}{t}")
             for j in range(PACK):
                 nc.tensor.transpose(p_turned[:, j, :], p_tiles[b, t][:, j * P : (j + 1) * P], identity[:])
+            return p_turned
+
+        def grouped_w(b, t):
             w_in[b, t] = sbuf([P, P, PACK], BF16, f"w_in{t}")
+            return w_in[b, t][:].rearrange("p (c i) j -> p c j i", i=RUN)
+
+        def weigh_on_vector(b, t):
+            p_turned = turn_p(b, t)
             scales = vs_columns[:, PACK * b : PACK * (b + 1)].unsqueeze(1).unsqueeze(3)
             nc.vector.tensor_tensor(
-                w_in[b, t][:].rearrange("p (c i) j -> p c j i", i=RUN),
+                grouped_w(b, t),
                 p_turned[:].rearrange("p j (c i) -> p c j i", i=RUN),
                 scales.to_broadcast([P, P // RUN, PACK, RUN]),
                 MULT,
             )
 
+        def weigh_on_scalar(b, t, blocks):
+            p_turned = turn_p(b, t)
+            for j in range(PACK):
+                n = PACK * b + j
+                nc.scalar.activation(blocks[:, j, :], p_turned[:, j, :], COPY, scale=vs_columns[:, n : n + 1])
+
+        def group_w(b, t, blocks):
+            nc.scalar.copy(grouped_w(b, t), blocks[:].rearrange("p j (c i) -> p c j i", i=RUN))
+
         def quant_w(b, t):
             cols = slice(t * P, (t + 1) * P)
             quantize(w_codes[b][:, cols], w_scales[b][:, cols], w_in[b, t][:].rearrange("p c j -> p (c j)"))
 
-        def gather_v(copy, window, e, b, place):
-            v_got[b, e] = sbuf([P, 2, N // 2], BF16, place)
-            copy(v_got[b, e][:].rearrange("p u (s r) -> p s u r", r=2), window[:].indirect(entries(b)))
+        def gather_v(e, b, tile):
+            v_got[b, e] = tile
+            nc.vector.tensor_copy(tile[:], v_pool[e][:].indirect(entries(b)))
 
-        def turn_v(b):
-            v_turned = psum.tile([P, 2, 2, P], F32, name="v_turned", tag=f"turn1{b}")
+        def turn_v(b, grouped):
+            v_turned = psum.tile([P, 2, 2, P], F32, name="v_turned", tag=f"turn0{b}")
             for e in range(2):
                 words = v_got[b, e][:].bitcast(F32)
                 for u in range(2):
-                    nc.tensor.transpose(v_turned[:, e, u, :], words[:, u, :], identity[:])
-            v_in[b] = sbuf([P, DV * PACK], BF16, f"minus_c1{b}")
+                    nc.tensor.transpose(v_turned[:, e, u, :], words[:, u : N // 2 : 2], identity[:])
+            v_in[b] = grouped
             nc.scalar.copy(
                 v_in[b][:].bitcast(F32).rearrange("p (e c i u) -> p e c u i", e=2, i=2, u=2),
                 v_turned[:].rearrange("p e u (c i) -> p e c u i", i=2),
@@ -217,58 +241,62 @@ def tile_attend_x_ks_cap_kernel(tc, qT, kT, vT, ks, vs, offs, out):
             divide(y[:], sums[:], inverse[:, 2 * b + t : 2 * b + t + 1])
             nc.sync.dma_start(out[b, cols, :], y[:])
 
-        cast_k(activation_copy, 0, 0, 0, CHUNK)
-        cast_k(nc.scalar.copy, 0, 1, 0, CHUNK)
+        cast_k(activation_copy, 0, 0)
+        cast_k(nc.scalar.copy, 0, 1)
         nc.vector.tensor_copy(vs_got[:], vs_pool[:].indirect(offsets[:]))
         vs_turned = turn_scales(vs_got, "turn10")
         nc.vector.tensor_copy(ks_got[:], ks_pool[:].indirect(offsets[:]))
         ks_turned = turn_scales(ks_got, "turn01")
         for b in range(B):
             gather_k(0, b)
-        cast_k(nc.scalar.copy, 1, 0, 0, CHUNK)
-        cast_k(nc.scalar.copy, 1, 1, 0, SPLIT)
-        cast_k(nc.vector.tensor_copy, 1, 1, SPLIT, CHUNK)
+        cast_k(nc.scalar.copy, 1, 0)
+        cast_k(nc.vector.tensor_copy, 1, 1)
+        cast_k(nc.scalar.copy, 1, 2, hi=SPLIT)
+        cast_k(nc.vector.tensor_copy, 1, 2, lo=SPLIT)
 
         for b in range(B):
             gather_k(1, b)
-        group_q(0, "k_raw11")
-        group_k(nc.vector.tensor_copy, 0, "q_raw0")
+        group_q(0, "k_raw12")
+        k_in = [sbuf([P, N * PACK], BF16, "k_in0"), placed(query_bytes, 2 * KIB, [P, N * PACK], BF16, "k_in1")]
+        group_k(nc.vector.tensor_copy, 0, slice(0, PACK))
         group_q(1, "q_in1")
-        group_k(nc.scalar.copy, 1, "k_in1")
+        group_k(nc.scalar.copy, 1, slice(2, PACK))
         half_ks = scale_columns(ks_turned, 1.0 / CAP, "k_pair1")
         vs_columns = scale_columns(vs_turned, 1.0, "q_raw1")
         quant_q(0)
-        quant_k(0, 2)
+        for g in range(2):
+            quant_k(0, g, placed(query_bytes, g * KIB, [P, N // 2], U32, f"k_codes0{g}"))
         scores(0)
+        group_k(nc.vector.tensor_copy, 1, slice(0, 2))
         quant_q(1)
-        quant_k(1, 1)
+        for g in range(2):
+            quant_k(1, g, sbuf([P, N // 2], U32, f"k_codes1{g}"))
         scores(1)
 
-        v_half = sbuf([P, T], BF16, "k_in1")
-        nc.vector.tensor_copy(v_half[:], v_pool[0][:])
-        gather_v(activation_copy, v_half, 0, 0, "k_pair1")
-        gather_v(nc.vector.tensor_copy, v_pool[1], 1, 0, "v_got")
-        for t in range(2):
-            soften(0, t)
-        gather_v(activation_copy, v_half, 0, 1, "minus_c01")
-        for t in range(2):
-            soften(1, t)
-        turn_v(0)
-        gather_v(nc.vector.tensor_copy, v_pool[1], 1, 1, "minus_c00")
+        for b in range(B):
+            gather_v(0, b, placed(query_bytes, (2 + b) * KIB, [P, N], BF16, f"v_got{b}0"))
+        gather_v(1, 0, sbuf([P, N], BF16, "v_got01"))
+        for b, t in ((0, 0), (0, 1), (1, 0)):
+            soften(b, t, sbuf([P, N], F32, f"minus_c{b}{t}"))
+        soften(1, 1, placed(last_bytes, 0, [P, N], F32, "minus_c11"))
+        gather_v(1, 1, sbuf([P, N], BF16, "minus_c01"))
 
         for t in range(2):
-            weigh(0, t)
-        turn_v(1)
+            weigh_on_vector(0, t)
+        turn_v(0, placed(last_bytes, KIB, [P, DV * PACK], BF16, "v_in0"))
+        w_blocks = placed(last_bytes, 0, [P, PACK, P], BF16, "w_blocks")
+        weigh_on_scalar(1, 0, w_blocks)
+        turn_v(1, sbuf([P, DV * PACK], BF16, "v_in1"))
+        group_w(1, 0, w_blocks)
         for t in range(2):
             quant_w(0, t)
-        weigh(1, 0)
         nc.vector.reciprocal(inverse[:], total[:])
         quant_v(0)
-        for t in range(2):
-            product(divide_on_scalar, 0, t)
-        weigh(1, 1)
-        quant_w(1, 0)
+        weigh_on_vector(1, 1)
         quant_v(1)
         quant_w(1, 1)
-        product(divide_on_scalar, 1, 0)
+        quant_w(1, 0)
+        for t in range(2):
+            product(divide_on_scalar, 0, t)
         product(divide_on_vector, 1, 1)
+        product(divide_on_scalar, 1, 0)

@@ -55,8 +55,9 @@ def tile_attend_x_ks_cap_kernel(tc, qT, kT, vT, ks, vs, offs, out):
 
         k_rows = kT.rearrange("(p h r) w -> p h r w", h=2, r=2)
         k_raw = [
-            [sbuf([P, 2, hi - lo], F32, f"k_raw{h}{c}") for c, (lo, hi) in enumerate(CHUNKS[h])] for h in range(2)
+            [sbuf([P, 2, hi - lo], F32, f"k_raw{h}{c}") for c, (lo, hi) in enumerate(CHUNKS[h][:2])] for h in range(2)
         ]
+        k_raw[1].append(placed(query_bytes, 4 * KIB, [P, 2, T // 4], F32, "k_raw12"))
         q_raw = [placed(query_bytes, 0, [P, PACK, NQ], F32, "q_raw0"), sbuf([P, PACK, NQ], F32, "q_raw1")]
         v_pool = [sbuf([P, T], F32, f"v_pool{e}") for e in range(2)]
         k_pair = [sbuf([P, 2 * T], BF16, f"k_pair{h}") for h in range(2)]
@@ -116,8 +117,7 @@ def tile_attend_x_ks_cap_kernel(tc, qT, kT, vT, ks, vs, offs, out):
                 nc.tensor.transpose(turned[:, 2 * n : 2 * n + P], got[:, b * N + j : (b + 1) * N : PACK], identity[:])
             return turned
 
-        def scale_columns(turned, factor, place):
-            columns = sbuf([P, B * PACK], F32, place)
+        def scale_columns(turned, factor, columns):
             nc.scalar.activation(columns[:], turned[:, 0 : 2 * B * PACK : 2], COPY, scale=factor)
             return columns
 
@@ -137,8 +137,8 @@ def tile_attend_x_ks_cap_kernel(tc, qT, kT, vT, ks, vs, offs, out):
             got = k_got[b][:].rearrange("p h (s j) -> p s j h", j=PACK)
             copy(words[:, :, blocks, :], got[:, :, blocks, :])
 
-        def group_q(b, place):
-            q_in[b] = sbuf([P, NQ, PACK], BF16, place)
+        def group_q(b, grouped):
+            q_in[b] = grouped
             nc.scalar.copy(
                 q_in[b][:].rearrange("p (c i) j -> p c j i", i=RUN),
                 q_raw[b][:].rearrange("p j (c i) -> p c j i", i=RUN),
@@ -256,13 +256,13 @@ def tile_attend_x_ks_cap_kernel(tc, qT, kT, vT, ks, vs, offs, out):
 
         for b in range(B):
             gather_k(1, b)
-        group_q(0, "k_raw12")
+        half_ks = scale_columns(ks_turned, 1.0 / CAP, placed(query_bytes, 6 * KIB, [P, B * PACK], F32, "half_ks"))
+        vs_columns = scale_columns(vs_turned, 1.0, placed(query_bytes, 7 * KIB, [P, B * PACK], F32, "vs_columns"))
+        group_q(0, placed(query_bytes, 4 * KIB, [P, NQ, PACK], BF16, "q_in0"))
         k_in = [sbuf([P, N * PACK], BF16, "k_in0"), placed(query_bytes, 2 * KIB, [P, N * PACK], BF16, "k_in1")]
         group_k(nc.vector.tensor_copy, 0, slice(0, PACK))
-        group_q(1, "q_in1")
+        group_q(1, sbuf([P, NQ, PACK], BF16, "q_in1"))
         group_k(nc.scalar.copy, 1, slice(2, PACK))
-        half_ks = scale_columns(ks_turned, 1.0 / CAP, "k_pair1")
-        vs_columns = scale_columns(vs_turned, 1.0, "q_raw1")
         quant_q(0)
         for g in range(2):
             quant_k(0, g, placed(query_bytes, g * KIB, [P, N // 2], U32, f"k_codes0{g}"))

@@ -182,15 +182,15 @@ def tile_attend_x_ks_cap_kernel(tc, qT, kT, vT, ks, vs, offs, out):
 
         def grouped_w(b, t):
             w_in[b, t] = sbuf([P, P, PACK], BF16, f"w_in{t}")
-            return w_in[b, t][:].rearrange("p (c i) j -> p c j i", i=RUN)
+            return w_in[b, t]
 
         def weigh_on_vector(b, t):
             p_turned = turn_p(b, t)
-            scales = vs_columns[:, PACK * b : PACK * (b + 1)].unsqueeze(1).unsqueeze(3)
+            scales = vs_columns[:, PACK * b : PACK * (b + 1)].unsqueeze(1)
             nc.vector.tensor_tensor(
-                grouped_w(b, t),
-                p_turned[:].rearrange("p j (c i) -> p c j i", i=RUN),
-                scales.to_broadcast([P, P // RUN, PACK, RUN]),
+                grouped_w(b, t)[:],
+                p_turned[:].rearrange("p j c -> p c j"),
+                scales.to_broadcast([P, P, PACK]),
                 MULT,
             )
 
@@ -201,7 +201,7 @@ def tile_attend_x_ks_cap_kernel(tc, qT, kT, vT, ks, vs, offs, out):
                 nc.scalar.activation(blocks[:, j, :], p_turned[:, j, :], COPY, scale=vs_columns[:, n : n + 1])
 
         def group_w(b, t, blocks):
-            nc.scalar.copy(grouped_w(b, t), blocks[:].rearrange("p j (c i) -> p c j i", i=RUN))
+            nc.scalar.copy(grouped_w(b, t)[:].rearrange("p (c i) j -> p c j i", i=RUN), blocks[:].rearrange("p j (c i) -> p c j i", i=RUN))
 
         def quant_w(b, t):
             cols = slice(t * P, (t + 1) * P)

@@ -9,8 +9,8 @@ PACK = 4
 CAP = 2.0
 RUN = 4
 KIB = 1024
-CHUNKS = (((0, T // 2), (T // 2, T)), ((0, T // 2), (T // 2, 3 * T // 4), (3 * T // 4, T)))
-SPLIT = 192
+CUTS = ((0, 3 * T // 2, 2 * T), (0, 3 * T // 2, 7 * T // 4, 2 * T))
+SHARE = 3 / 8
 
 FLOPS = 2 * B * NQ * N * (D + DV)
 BYTES = 4 * (B * D * NQ + D * T + DV * T + 2 * T + B * NQ * DV) + 2 * B * N * P // 16
@@ -48,29 +48,27 @@ def tile_attend_x_ks_cap_kernel(tc, qT, kT, vT, ks, vs, offs, out):
 
         ks_pool = sbuf([P, T], F32, "ks_pool")
         vs_pool = sbuf([P, T], F32, "vs_pool")
+        nc.vector.memset(vs_pool[:], 0.0)
         nc.vector.memset(ks_pool[:], 0.0)
-        nc.gpsimd.memset(vs_pool[:], 0.0)
         identity = sbuf([P, P], F32, "identity")
         make_identity(nc, identity[:])
 
-        k_rows = kT.rearrange("(p h r) w -> p h r w", h=2, r=2)
-        k_raw = [
-            [sbuf([P, 2, hi - lo], F32, f"k_raw{h}{c}") for c, (lo, hi) in enumerate(CHUNKS[h][:2])] for h in range(2)
-        ]
-        k_raw[1].append(placed(query_bytes, 4 * KIB, [P, 2, T // 4], F32, "k_raw12"))
+        k_rows = kT.rearrange("(p h r) w -> p h (r w)", h=2, r=2)
+        k_raw = [sbuf([P, 2 * T], F32, "k_raw0"), placed(query_bytes, 4 * KIB, [P, 2 * T], F32, "k_raw1")]
         q_raw = [placed(query_bytes, 0, [P, PACK, NQ], F32, "q_raw0"), sbuf([P, PACK, NQ], F32, "q_raw1")]
         v_pool = [sbuf([P, T], F32, f"v_pool{e}") for e in range(2)]
         k_pair = [sbuf([P, 2 * T], BF16, f"k_pair{h}") for h in range(2)]
 
         def load_k(h, c):
-            nc.sync.dma_start(k_raw[h][c][:], k_rows[:, h, :, CHUNKS[h][c][0] : CHUNKS[h][c][1]])
+            cut = slice(CUTS[h][c], CUTS[h][c + 1])
+            nc.sync.dma_start(k_raw[h][:, cut], k_rows[:, h, cut])
 
-        load_k(0, 0)
         nc.sync.dma_start(offsets[:], offs)
+        load_k(0, 0)
         nc.scalar.dma_start(vs_pool[0:1, :], vs[0:1, :])
-        load_k(0, 1)
         nc.sync.dma_start(ks_pool[0:1, :], ks[0:1, :])
-        for c in range(len(CHUNKS[1])):
+        load_k(0, 1)
+        for c in range(len(CUTS[1]) - 1):
             load_k(1, c)
         for b in range(B):
             nc.sync.dma_start(q_raw[b][:], qT[b].rearrange("(p j) w -> p j w", j=PACK))
@@ -121,13 +119,16 @@ def tile_attend_x_ks_cap_kernel(tc, qT, kT, vT, ks, vs, offs, out):
             nc.scalar.activation(columns[:], turned[:, 0 : 2 * B * PACK : 2], COPY, scale=factor)
             return columns
 
-        def cast_k(copy, h, c, lo=0, hi=None):
-            first, end = CHUNKS[h][c]
-            hi = end - first if hi is None else hi
+        def cast_k(copy, h, lo, hi):
             copy(
-                k_pair[h][:, 2 * (first + lo) : 2 * (first + hi)].rearrange("p (w i r) -> p w r i", i=RUN, r=2),
-                k_raw[h][c][:, :, lo:hi].rearrange("p r (w i) -> p w r i", i=RUN),
+                k_pair[h][:, 2 * lo : 2 * hi].rearrange("p (w i r) -> p w r i", i=RUN, r=2),
+                k_raw[h][:].rearrange("p (r t) -> p r t", r=2)[:, :, lo:hi].rearrange("p r (w i) -> p w r i", i=RUN),
             )
+
+        def cast_shared(h, lo, hi):
+            middle = lo + int(SHARE * (hi - lo))
+            cast_k(nc.scalar.copy, h, lo, middle)
+            cast_k(nc.vector.tensor_copy, h, middle, hi)
 
         def gather_k(h, b):
             nc.vector.tensor_copy(k_got[b][:, h, :], k_pair[h][:].bitcast(U32).indirect(entries(b)))
@@ -241,18 +242,18 @@ def tile_attend_x_ks_cap_kernel(tc, qT, kT, vT, ks, vs, offs, out):
             divide(y[:], sums[:], inverse[:, 2 * b + t : 2 * b + t + 1])
             nc.sync.dma_start(out[b, cols, :], y[:])
 
-        cast_k(activation_copy, 0, 0)
-        cast_k(nc.scalar.copy, 0, 1)
+        cast_k(activation_copy, 0, 0, T // 2)
         nc.vector.tensor_copy(vs_got[:], vs_pool[:].indirect(offsets[:]))
         vs_turned = turn_scales(vs_got, "turn10")
         nc.vector.tensor_copy(ks_got[:], ks_pool[:].indirect(offsets[:]))
         ks_turned = turn_scales(ks_got, "turn01")
+        cast_k(nc.scalar.copy, 0, T // 2, 5 * T // 8)
+        cast_k(nc.vector.tensor_copy, 0, 5 * T // 8, T)
         for b in range(B):
             gather_k(0, b)
-        cast_k(nc.scalar.copy, 1, 0)
-        cast_k(nc.vector.tensor_copy, 1, 1)
-        cast_k(nc.scalar.copy, 1, 2, hi=SPLIT)
-        cast_k(nc.vector.tensor_copy, 1, 2, lo=SPLIT)
+        cast_shared(1, 0, T // 2)
+        cast_shared(1, T // 2, 3 * T // 4)
+        cast_shared(1, 3 * T // 4, T)
 
         for b in range(B):
             gather_k(1, b)

from contextlib import ExitStack

import concourse.mybir as mybir
from concourse.masks import make_identity

B, N, T, D, DV, NQ = 2, 512, 2048, 512, 256, 256
P = 128
PACK = 4
CAP = 2.0
RUN = 4
KIB = 1024
CUTS = ((0, 3 * T // 2, 2 * T), (0, 3 * T // 2, 7 * T // 4, 2 * T))
SHARE = 3 / 8

FLOPS = 2 * B * NQ * N * (D + DV)
BYTES = 4 * (B * D * NQ + D * T + DV * T + 2 * T + B * NQ * DV) + 2 * B * N * P // 16

F32 = mybir.dt.float32
BF16 = mybir.dt.bfloat16
U32 = mybir.dt.uint32
U16 = mybir.dt.uint16
U8 = mybir.dt.uint8
FP8X4 = mybir.dt.float8_e4m3fn_x4

MULT = mybir.AluOpType.mult
MIN = mybir.AluOpType.min
COPY = mybir.ActivationFunctionType.Copy
EXP = mybir.ActivationFunctionType.Exp
TANH = mybir.ActivationFunctionType.Tanh


def tile_attend_x_ks_cap_kernel(tc, qT, kT, vT, ks, vs, offs, out):
    nc = tc.nc
    with ExitStack() as ctx:
        held = ctx.enter_context(tc.tile_pool(name="held", bufs=1))
        psum = ctx.enter_context(tc.psum_pool(name="psum", bufs=1))

        query_bytes = ctx.enter_context(tc.tile_pool(name="query_bytes", bufs=1))
        last_bytes = ctx.enter_context(tc.tile_pool(name="last_bytes", bufs=1))

        def placed(pool, offset, shape, dtype, name):
            return pool.tile(shape, dtype, name=name, tag=name, align_bytes=64, offset=offset)

        def sbuf(shape, dtype, place):
            return held.tile(shape, dtype, name=place, tag=place, align_bytes=64)

        offsets = held.tile([P, B * N // 16], U16, name="offsets")

        ks_pool = sbuf([P, T], F32, "ks_pool")
        vs_pool = sbuf([P, T], F32, "vs_pool")
        nc.vector.memset(vs_pool[:], 0.0)
        nc.vector.memset(ks_pool[:], 0.0)
        identity = sbuf([P, P], F32, "identity")
        make_identity(nc, identity[:])

        k_rows = kT.rearrange("(p h r) w -> p h (r w)", h=2, r=2)
        k_raw = [sbuf([P, 2 * T], F32, "k_raw0"), placed(query_bytes, 4 * KIB, [P, 2 * T], F32, "k_raw1")]
        q_raw = [placed(query_bytes, 0, [P, PACK, NQ], F32, "q_raw0"), sbuf([P, PACK, NQ], F32, "q_raw1")]
        v_pool = [sbuf([P, T], F32, f"v_pool{e}") for e in range(2)]
        k_pair = [sbuf([P, 2 * T], BF16, f"k_pair{h}") for h in range(2)]

        def load_k(h, c):
            cut = slice(CUTS[h][c], CUTS[h][c + 1])
            nc.sync.dma_start(k_raw[h][:, cut], k_rows[:, h, cut])

        nc.sync.dma_start(offsets[:], offs)
        load_k(0, 0)
        nc.scalar.dma_start(vs_pool[0:1, :], vs[0:1, :])
        nc.sync.dma_start(ks_pool[0:1, :], ks[0:1, :])
        load_k(0, 1)
        for c in range(len(CUTS[1]) - 1):
            load_k(1, c)
        for b in range(B):
            nc.sync.dma_start(q_raw[b][:], qT[b].rearrange("(p j) w -> p j w", j=PACK))
        for e in range(2):
            nc.sync.dma_start(v_pool[e][:], vT[e * P : (e + 1) * P, :])

        total = sbuf([P, 2 * B], F32, "total")
        inverse = sbuf([P, 2 * B], F32, "inverse")
        k_got = [sbuf([P, 2, N], U32, f"k_got{b}") for b in range(B)]
        q_codes = [sbuf([P, NQ], U32, f"q_codes{b}") for b in range(B)]
        w_codes = [sbuf([P, NQ], U32, f"w_codes{b}") for b in range(B)]
        q_scales = [sbuf([P, NQ], U8, f"q_scales{b}") for b in range(B)]
        k_scales = [sbuf([P, N], U8, f"k_scales{b}") for b in range(B)]
        w_scales = [sbuf([P, NQ], U8, f"w_scales{b}") for b in range(B)]
        v_scales = [sbuf([P, DV], U8, f"v_scales{b}") for b in range(B)]
        ks_got = sbuf([P, B * N], F32, "ks_got")
        vs_got = sbuf([P, B * N], F32, "vs_got")
        k_codes, q_in, v_in, v_codes, capped, p_tiles, w_in, v_got = {}, {}, {}, {}, {}, {}, {}, {}

        def entries(b):
            return offsets[:, b * (N // 16) : (b + 1) * (N // 16)]

        def quantize(codes, scales, grouped):
            nc.vector.quantize_mx(out=codes.bitcast(FP8X4), scales=scales, in_=grouped)

        def multiply(sums, lhs_codes, lhs_scales, rhs_codes, rhs_scales):
            nc.tensor.matmul_mx(
                out=sums,
                lhsT=lhs_codes.bitcast(FP8X4),
                lhsT_scale=lhs_scales,
                rhs=rhs_codes.bitcast(FP8X4),
                rhs_scale=rhs_scales,
                start=True,
                stop=True,
            )

        def activation_copy(dst, src):
            nc.scalar.activation(dst, src, COPY)

        def turn_scales(got, bank):
            turned = psum.tile([P, P + 2 * B * PACK], F32, name="turned", tag=bank)
            for n in range(B * PACK):
                b, j = divmod(n, PACK)
                nc.tensor.transpose(turned[:, 2 * n : 2 * n + P], got[:, b * N + j : (b + 1) * N : PACK], identity[:])
            return turned

        def scale_columns(turned, factor, columns):
            nc.scalar.activation(columns[:], turned[:, 0 : 2 * B * PACK : 2], COPY, scale=factor)
            return columns

        def cast_k(copy, h, lo, hi):
            copy(
                k_pair[h][:, 2 * lo : 2 * hi].rearrange("p (w i r) -> p w r i", i=RUN, r=2),
                k_raw[h][:].rearrange("p (r t) -> p r t", r=2)[:, :, lo:hi].rearrange("p r (w i) -> p w r i", i=RUN),
            )

        def cast_shared(h, lo, hi):
            middle = lo + int(SHARE * (hi - lo))
            cast_k(nc.scalar.copy, h, lo, middle)
            cast_k(nc.vector.tensor_copy, h, middle, hi)

        def gather_k(h, b):
            nc.vector.tensor_copy(k_got[b][:, h, :], k_pair[h][:].bitcast(U32).indirect(entries(b)))

        def group_k(copy, b, blocks):
            words = k_in[b][:].bitcast(U32).rearrange("p (j s h) -> p s j h", j=PACK, h=2)
            got = k_got[b][:].rearrange("p h (s j) -> p s j h", j=PACK)
            copy(words[:, :, blocks, :], got[:, :, blocks, :])

        def group_q(b, grouped):
            q_in[b] = grouped
            nc.scalar.copy(
                q_in[b][:].rearrange("p (c i) j -> p c j i", i=RUN),
                q_raw[b][:].rearrange("p j (c i) -> p c j i", i=RUN),
            )

        def quant_q(b):
            quantize(q_codes[b][:], q_scales[b][:], q_in[b][:].rearrange("p c j -> p (c j)"))

        def quant_k(b, g, codes):
            k_codes[b, g] = codes
            cols = slice(g * N // 2, (g + 1) * N // 2)
            quantize(codes[:], k_scales[b][:, cols], k_in[b][:, PACK * cols.start : PACK * cols.stop])

        def scores(b):
            capped[b] = sbuf([P, PACK, NQ], F32, f"capped{b}")
            for g in range(2):
                sums = psum.tile([P, 2, NQ], F32, name="sums", tag=f"product{b}{g}")
                for i in range(2):
                    cols = slice((2 * g + i) * P, (2 * g + i + 1) * P)
                    codes = k_codes[b, g][:, i * P : (i + 1) * P]
                    multiply(sums[:, i, :], codes, k_scales[b][:, cols], q_codes[b][:], q_scales[b][:])
                for i in range(2):
                    n = PACK * b + 2 * g + i
                    nc.scalar.activation(capped[b][:, 2 * g + i, :], sums[:, i, :], TANH, scale=half_ks[:, n : n + 1])

        def soften(b, t, minus_c):
            rows = psum.tile([P, N], F32, name="rows", tag=f"turn{b}{t}")
            for j in range(PACK):
                nc.tensor.transpose(rows[:, j * P : (j + 1) * P], capped[b][:, j, t * P : (t + 1) * P], identity[:])
            minus_m = sbuf([P, 1], F32, f"minus_m{b}{t}")
            nc.vector.tensor_scalar(minus_c[:], rows[:], -CAP, None, MULT, MIN, accum_out=minus_m[:])
            p_tiles[b, t] = sbuf([P, N], F32, f"p{b}{t}")
            row_sum = total[:, 2 * b + t : 2 * b + t + 1]
            nc.scalar.activation(p_tiles[b, t][:], minus_c[:], EXP, bias=minus_m[:], scale=-1.0, accum_out=row_sum)

        def turn_p(b, t):
            p_turned = psum.tile([P, PACK, P], F32, name="p_turned", tag=f"product{b}{t}")
            for j in range(PACK):
                nc.tensor.transpose(p_turned[:, j, :], p_tiles[b, t][:, j * P : (j + 1) * P], identity[:])
            return p_turned

        def grouped_w(b, t):
            w_in[b, t] = sbuf([P, P, PACK], BF16, f"w_in{t}")
            return w_in[b, t]

        def weigh_on_vector(b, t):
            p_turned = turn_p(b, t)
            scales = vs_columns[:, PACK * b : PACK * (b + 1)].unsqueeze(1)
            nc.vector.tensor_tensor(
                grouped_w(b, t)[:],
                p_turned[:].rearrange("p j c -> p c j"),
                scales.to_broadcast([P, P, PACK]),
                MULT,
            )

        def weigh_on_scalar(b, t, blocks):
            p_turned = turn_p(b, t)
            for j in range(PACK):
                n = PACK * b + j
                nc.scalar.activation(blocks[:, j, :], p_turned[:, j, :], COPY, scale=vs_columns[:, n : n + 1])

        def group_w(b, t, blocks):
            nc.scalar.copy(grouped_w(b, t)[:].rearrange("p (c i) j -> p c j i", i=RUN), blocks[:].rearrange("p j (c i) -> p c j i", i=RUN))

        def quant_w(b, t):
            cols = slice(t * P, (t + 1) * P)
            quantize(w_codes[b][:, cols], w_scales[b][:, cols], w_in[b, t][:].rearrange("p c j -> p (c j)"))

        def gather_v(e, b, tile):
            v_got[b, e] = tile
            nc.vector.tensor_copy(tile[:], v_pool[e][:].indirect(entries(b)))

        def turn_v(b, grouped):
            v_turned = psum.tile([P, 2, 2, P], F32, name="v_turned", tag=f"turn0{b}")
            for e in range(2):
                words = v_got[b, e][:].bitcast(F32)
                for u in range(2):
                    nc.tensor.transpose(v_turned[:, e, u, :], words[:, u : N // 2 : 2], identity[:])
            v_in[b] = grouped
            nc.scalar.copy(
                v_in[b][:].bitcast(F32).rearrange("p (e c i u) -> p e c u i", e=2, i=2, u=2),
                v_turned[:].rearrange("p e u (c i) -> p e c u i", i=2),
            )

        def quant_v(b):
            v_codes[b] = sbuf([P, DV], U32, f"p1{b}")
            quantize(v_codes[b][:], v_scales[b][:], v_in[b][:])

        def divide_on_scalar(dst, sums, factor):
            nc.scalar.activation(dst, sums, COPY, scale=factor)

        def divide_on_vector(dst, sums, factor):
            nc.vector.tensor_scalar(dst, sums, factor, None, MULT)

        def product(divide, b, t):
            cols = slice(t * P, (t + 1) * P)
            sums = psum.tile([P, DV], F32, name="sums", tag=f"product{b}{t}")
            multiply(sums[:], w_codes[b][:, cols], w_scales[b][:, cols], v_codes[b][:], v_scales[b][:])
            y = sbuf([P, DV], F32, f"y{b}{t}")
            divide(y[:], sums[:], inverse[:, 2 * b + t : 2 * b + t + 1])
            nc.sync.dma_start(out[b, cols, :], y[:])

        cast_k(activation_copy, 0, 0, T // 2)
        nc.vector.tensor_copy(vs_got[:], vs_pool[:].indirect(offsets[:]))
        vs_turned = turn_scales(vs_got, "turn10")
        nc.vector.tensor_copy(ks_got[:], ks_pool[:].indirect(offsets[:]))
        ks_turned = turn_scales(ks_got, "turn01")
        cast_k(nc.scalar.copy, 0, T // 2, 5 * T // 8)
        cast_k(nc.vector.tensor_copy, 0, 5 * T // 8, T)
        for b in range(B):
            gather_k(0, b)
        cast_shared(1, 0, T // 2)
        cast_shared(1, T // 2, 3 * T // 4)
        cast_shared(1, 3 * T // 4, T)

        for b in range(B):
            gather_k(1, b)
        half_ks = scale_columns(ks_turned, 1.0 / CAP, placed(query_bytes, 6 * KIB, [P, B * PACK], F32, "half_ks"))
        vs_columns = scale_columns(vs_turned, 1.0, placed(query_bytes, 7 * KIB, [P, B * PACK], F32, "vs_columns"))
        group_q(0, placed(query_bytes, 4 * KIB, [P, NQ, PACK], BF16, "q_in0"))
        k_in = [sbuf([P, N * PACK], BF16, "k_in0"), placed(query_bytes, 2 * KIB, [P, N * PACK], BF16, "k_in1")]
        group_k(nc.vector.tensor_copy, 0, slice(0, PACK))
        group_q(1, sbuf([P, NQ, PACK], BF16, "q_in1"))
        group_k(nc.scalar.copy, 1, slice(2, PACK))
        quant_q(0)
        for g in range(2):
            quant_k(0, g, placed(query_bytes, g * KIB, [P, N // 2], U32, f"k_codes0{g}"))
        scores(0)
        group_k(nc.vector.tensor_copy, 1, slice(0, 2))
        quant_q(1)
        for g in range(2):
            quant_k(1, g, sbuf([P, N // 2], U32, f"k_codes1{g}"))
        scores(1)

        for b in range(B):
            gather_v(0, b, placed(query_bytes, (2 + b) * KIB, [P, N], BF16, f"v_got{b}0"))
        gather_v(1, 0, sbuf([P, N], BF16, "v_got01"))
        for b, t in ((0, 0), (0, 1), (1, 0)):
            soften(b, t, sbuf([P, N], F32, f"minus_c{b}{t}"))
        soften(1, 1, placed(last_bytes, 0, [P, N], F32, "minus_c11"))
        gather_v(1, 1, sbuf([P, N], BF16, "minus_c01"))

        for t in range(2):
            weigh_on_vector(0, t)
        turn_v(0, placed(last_bytes, KIB, [P, DV * PACK], BF16, "v_in0"))
        w_blocks = placed(last_bytes, 0, [P, PACK, P], BF16, "w_blocks")
        weigh_on_scalar(1, 0, w_blocks)
        turn_v(1, sbuf([P, DV * PACK], BF16, "v_in1"))
        group_w(1, 0, w_blocks)
        for t in range(2):
            quant_w(0, t)
        nc.vector.reciprocal(inverse[:], total[:])
        quant_v(0)
        weigh_on_vector(1, 1)
        quant_v(1)
        quant_w(1, 1)
        quant_w(1, 0)
        for t in range(2):
            product(divide_on_scalar, 0, t)
        product(divide_on_vector, 1, 1)
        product(divide_on_scalar, 1, 0)
